import numpy as np
import ml_dtypes


def mxq(x, axis, fmt="e4m3"):
    dtype, down = {"e4m3": (ml_dtypes.float8_e4m3fn, 7), "e5m2": (ml_dtypes.float8_e5m2, 14)}[fmt]
    v = np.moveaxis(np.asarray(x, np.float32).astype(ml_dtypes.bfloat16).astype(np.float64), axis, -1)
    blocks = v.reshape(v.shape[:-1] + (-1, 32))
    amax = np.abs(blocks).max(-1, keepdims=True)
    byte = np.maximum(np.where(amax > 0, np.frexp(amax)[1] - 1 + 127, 0) - down, 1)
    scale = np.exp2(byte - 127.0)
    codes = (blocks / scale).astype(np.float32).astype(dtype).astype(np.float64)
    return np.moveaxis((codes * scale).reshape(v.shape), -1, axis)


WIDE = False


def mx_kscale(k):
    if not WIDE:
        return np.ones(k)
    levels = np.array([10, -10, 5, -5, 0])
    if k % 512:
        return np.exp2(np.random.permutation(np.resize(levels, k // 32))).repeat(32)
    a = np.empty((k // 512, 16))
    for p in range(k // 512):
        a[p, :8] = np.random.permutation(np.resize(levels, 8))
        for g in range(8):
            far = levels[np.abs(levels - a[p, g]) >= 10]
            a[p, g + 8] = far[np.random.randint(len(far))]
    return np.exp2(a.ravel()).repeat(32)


def f64(x):
    return np.asarray(x).astype(np.float64)


def striped(idx):
    return np.tile(idx.reshape(-1, 16).T, (8, 1)).astype(np.uint16)


def unstriped(offs):
    return offs[:16].T.reshape(-1).astype(np.int64)


def pack_weight(w):
    k, n = w.shape
    w = f64(np.asarray(w, np.float32).astype(ml_dtypes.bfloat16)).reshape(k // 32, 32, n)
    amax = np.abs(w).max(1)
    byte = np.clip(np.where(amax > 0, np.frexp(amax)[1] - 1 + 127 - 7, 1), 1, 254)
    scaled = (w * np.exp2(127.0 - byte)[:, None, :]).reshape(k, n).astype(np.float32)
    words = np.ascontiguousarray(scaled.reshape(k // 512, 128, 4, n).transpose(0, 1, 3, 2)).astype(ml_dtypes.float8_e4m3fn).view(np.uint8)
    return words, np.ascontiguousarray(byte.astype(np.uint8).reshape(k // 512, 16, n))


def unpack_weight(words, scales):
    g, p, n, _ = words.shape
    vals = np.ascontiguousarray(words).view(ml_dtypes.float8_e4m3fn).astype(np.float64) * np.repeat(np.exp2(scales.astype(np.float64) - 127.0), 8, axis=1)[..., None]
    return vals.transpose(0, 1, 3, 2).reshape(g * 512, n)


def silu(v):
    return v / (1.0 + np.exp(-np.maximum(v, -700.0)))

def planes(y):
    n, m = y.shape
    v = y.astype(np.float32).astype(ml_dtypes.bfloat16).astype(np.float64).reshape(n // 32, 32, m)
    top = np.abs(v).max(1)
    byte = np.clip(np.where(top > 0, np.frexp(top)[1] - 1 + 127 - 7, 1), 1, 254)
    codes = (v * np.exp2(127.0 - byte)[:, None, :]).reshape(n, m).astype(np.float32).astype(ml_dtypes.float8_e4m3fn).view(np.uint8)
    words = codes.reshape(n // 512, 128, 4, m).transpose(0, 1, 3, 2)
    return np.ascontiguousarray(words), np.ascontiguousarray(byte.astype(np.uint8).reshape(n // 512, 16, m))


K, T, S, V, H, J, U = 512, 2048, 512, 256, 512, 512, 512


def setup_inputs():
    n = np.random.standard_normal
    s = mx_kscale(K)[:, None]
    u = mx_kscale(H)
    r = mx_kscale(J)[:, None]
    packed_xT = pack_weight(n((K, T)) * s)
    packed_w2 = pack_weight(n((H, H)) / np.sqrt(2 * H) / u[:, None])
    return {
        "x_words": packed_xT[0],
        "x_scales": packed_xT[1],
        "aT": (n((J, U)) * r).astype(np.float32),
        "w1": (n((K, H)) / np.sqrt(K) / s * u).astype(np.float32),
        "w3": (n((J, H)) / np.sqrt(J) / r).astype(np.float32),
        "w2_words": packed_w2[0],
        "w2_scales": packed_w2[1],
        "offs": striped(np.random.permutation(T)[:S]),
        "pos1": striped(np.random.permutation(S)[:V]),
        "pos2": striped(np.random.permutation(S)[:V]),
    }


def reference(x_words, x_scales, aT, w1, w3, w2_words, w2_scales, offs, pos1, pos2):
    xq = unpack_weight(x_words, x_scales)[:, unstriped(offs)]
    h = silu(mxq(f64(w1), 0, "e4m3").T @ xq)
    f = mxq(f64(w3), 0, "e4m3").T @ mxq(f64(aT), 0, "e4m3")
    z = h[:, unstriped(pos1)] * f[:, :V] + h[:, unstriped(pos2)] * f[:, V:2 * V]
    out_0 = unpack_weight(w2_words, w2_scales).T @ mxq(z, 0, "e4m3")
    return (out_0,) + planes(out_0)

@@ -1,0 +1,203 @@
+from contextlib import ExitStack
+
+import concourse.mybir as mybir
+
+K, T, S, V, H, J, U = 512, 2048, 512, 256, 512, 512, 512
+FLOPS = 2 * K * H * S + 2 * J * H * U + 2 * H * H * V
+
+F32 = mybir.dt.float32
+BF16 = mybir.dt.bfloat16
+I32 = mybir.dt.int32
+U32 = mybir.dt.uint32
+U16 = mybir.dt.uint16
+U8 = mybir.dt.uint8
+FP8X4 = mybir.dt.float8_e4m3fn_x4
+MULT = mybir.AluOpType.mult
+ADD = mybir.AluOpType.add
+SILU = mybir.ActivationFunctionType.Silu
+
+P = 128
+PACK = 4
+HALF = 256
+HM = HALF // PACK
+
+
+def tile_picked_dime_none_po_kernel(
+    tc, x_words, x_scales, aT, w1, w3, w2_words, w2_scales, offs, pos1, pos2, out_0, out_1, out_2
+):
+    nc = tc.nc
+    with ExitStack() as ctx:
+        lists = ctx.enter_context(tc.tile_pool(name="lists", bufs=1))
+        sb = ctx.enter_context(tc.tile_pool(name="sb", bufs=1))
+        psum = ctx.enter_context(tc.psum_pool(name="psum", bufs=4))
+
+        def tile(shape, dtype, name):
+            return sb.tile(shape, dtype, name=name, align_bytes=64)
+
+        def load_half(pool, src, half, name):
+            raw = pool.tile([P, PACK, HALF], F32, name=name)
+            nc.sync.dma_start(
+                out=raw[:], in_=src.rearrange("(p j) c -> p j c", j=PACK)[:, :, half * HALF : (half + 1) * HALF]
+            )
+            return raw
+
+        def load_scale_rows(queue, plane, src):
+            for q in range(4):
+                queue.dma_start(
+                    out=plane[32 * q : 32 * q + 4, :].bitcast(I32), in_=src[0, 4 * q : 4 * q + 4, :].bitcast(I32)
+                )
+
+        def load_list(src, entries, name):
+            held = lists.tile([P, entries // 16], U16, name=name)
+            nc.sync.dma_start(held[:], src)
+            return held
+
+        def load_words(pool, src, columns, name):
+            words = pool.tile([P, columns], I32, name=name, align_bytes=64)
+            nc.sync.dma_start(out=words[:], in_=src[0].rearrange("p c r -> p (c r)").bitcast(I32))
+            return words
+
+        def round_dealt(copy, raw, name):
+            dealt = tile([P, PACK, HM, PACK], BF16, name)
+            copy(out=dealt[:].rearrange("p t m j -> p m j t"), in_=raw[:].rearrange("p j (m t) -> p m j t", t=PACK))
+            return dealt
+
+        def quantize_dealt(dealt, half, codes, scales):
+            for t in range(PACK):
+                cols = slice(t * P + half * HM, t * P + (half + 1) * HM)
+                nc.vector.quantize_mx(
+                    out=codes[:, cols].bitcast(FP8X4),
+                    scales=scales[:, cols],
+                    in_=dealt[:, t].rearrange("p m j -> p (m j)"),
+                )
+
+        def quantize(grouped, columns, name):
+            codes = tile([P, columns], U32, name + "_codes")
+            scales = tile([P, columns], U8, name + "_scales")
+            nc.vector.quantize_mx(
+                out=codes[:].bitcast(FP8X4), scales=scales[:], in_=grouped[:].rearrange("p c j -> p (c j)")
+            )
+            return codes, scales
+
+        def product(out, w_codes, w_scales, t, codes, scales):
+            cols = slice(t * P, (t + 1) * P)
+            nc.tensor.matmul_mx(
+                out=out,
+                lhsT=w_codes[:, cols].bitcast(FP8X4),
+                lhsT_scale=w_scales[:, cols],
+                rhs=codes[:].bitcast(FP8X4),
+                rhs_scale=scales[:],
+                start=True,
+                stop=True,
+            )
+
+        xs_all = tile([P, T], U8, "xs_all")
+        nc.vector.memset(xs_all[:].bitcast(I32), 0)
+        w2s_raw = tile([P, H], U8, "w2s_raw")
+        nc.vector.memset(w2s_raw[:].bitcast(I32), 0)
+        offs_t = load_list(offs, S, "offs_t")
+        pos_t = [load_list(pos1, V, "pos1_t"), load_list(pos2, V, "pos2_t")]
+        w1_codes = tile([P, H], U32, "w1_codes")
+        w1_scales = tile([P, H], U8, "w1_scales")
+        with tc.tile_pool(name="first", bufs=1) as first:
+            w1_raw0 = load_half(first, w1, 0, "w1_raw0")
+            load_scale_rows(nc.scalar, xs_all, x_scales)
+            xw_all = load_words(sb, x_words, T, "xw_all")
+            w1_bf0 = round_dealt(nc.vector.tensor_copy, w1_raw0, "w1_bf0")
+        load_scale_rows(nc.gpsimd, w2s_raw, w2_scales)
+        later = ctx.enter_context(tc.tile_pool(name="later", bufs=1))
+        w1_raw1 = load_half(later, w1, 1, "w1_raw1")
+        w3_raw = [load_half(later, w3, half, "w3_raw%d" % half) for half in range(2)]
+        a_raw = [load_half(later, aT, 0, "a_raw0")]
+        w2w_raw = load_words(later, w2_words, H, "w2w_raw")
+        a_raw.append(load_half(later, aT, 1, "a_raw1"))
+
+        quantize_dealt(w1_bf0, 0, w1_codes, w1_scales)
+        xs = tile([P, S], U8, "xs")
+        nc.vector.tensor_copy(out=xs[:], in_=xs_all[:].indirect(offs_t[:]))
+        xw = tile([P, S], U32, "xw")
+        nc.vector.tensor_copy(out=xw[:], in_=xw_all[:].bitcast(U32).indirect(offs_t[:]))
+        quantize_dealt(round_dealt(nc.vector.tensor_copy, w1_raw1, "w1_bf1"), 1, w1_codes, w1_scales)
+        h = []
+        for t in range(PACK):
+            acc = psum.tile([P, S], F32, name="wide", tag="wide")
+            product(acc[:], w1_codes, w1_scales, t, xw, xs)
+            h.append(tile([P, S], F32, "h%d" % t))
+            nc.scalar.activation(out=h[t][:], in_=acc[:], func=SILU)
+
+        w3_codes = tile([P, H], U32, "w3_codes")
+        w3_scales = tile([P, H], U8, "w3_scales")
+        for half in range(2):
+            quantize_dealt(round_dealt(nc.vector.tensor_copy, w3_raw[half], "w3_bf%d" % half), half, w3_codes, w3_scales)
+
+        def filters(d, copy):
+            grouped = tile([P, V, PACK], BF16, "a_bf%d" % d)
+            copy(
+                out=grouped[:].rearrange("p (c i) j -> p c j i", i=4),
+                in_=a_raw[d][:].rearrange("p j (c i) -> p c j i", i=4),
+            )
+            a_codes, a_scales = quantize(grouped, V, "a%d" % d)
+            f = []
+            for pair in range(2):
+                acc = psum.tile([P, 2, V], F32, name="pair", tag="pair")
+                for u in range(2):
+                    product(acc[:, u, :], w3_codes, w3_scales, 2 * pair + u, a_codes, a_scales)
+                held = tile([P, 2, V], F32, "f%d_%d" % (d, pair))
+                nc.scalar.copy(out=held[:], in_=acc[:])
+                f.extend([held[:, 0, :], held[:, 1, :]])
+            return f
+
+        def messages(d, f):
+            prod = tile([P, PACK, V], F32, "prod%d" % d)
+            for t in range(PACK):
+                nc.vector.tensor_tensor(out=prod[:, t, :], in0=h[t][:].indirect(pos_t[d][:]), in1=f[t], op=MULT)
+            return prod
+
+        f0 = filters(0, nc.vector.tensor_copy)
+
+        w2_codes = tile([P, H], I32, "w2_codes")
+        nc.vector.tensor_copy(
+            out=w2_codes[:].rearrange("p (t m) -> p m t", t=PACK), in_=w2w_raw[:].rearrange("p (m t) -> p m t", t=PACK)
+        )
+        w2_sc = tile([P, H], U8, "w2_sc")
+        nc.vector.tensor_copy(
+            out=w2_sc[:].rearrange("p (t m) -> p m t", t=PACK), in_=w2s_raw[:].rearrange("p (m t) -> p m t", t=PACK)
+        )
+
+        f1 = filters(1, nc.scalar.copy)
+        prods = [messages(0, f0), messages(1, f1)]
+
+        z = []
+        for half in range(2):
+            cols = slice(half * P, (half + 1) * P)
+            zb = tile([P, P, PACK], BF16, "z_bf%d" % half)
+            nc.vector.tensor_tensor(
+                out=zb[:].rearrange("p (c i) t -> p c t i", i=4),
+                in0=prods[0][:, :, cols].rearrange("p t (c i) -> p c t i", i=4),
+                in1=prods[1][:, :, cols].rearrange("p t (c i) -> p c t i", i=4),
+                op=ADD,
+            )
+            z.append(zb)
+        zq = [quantize(z[half], P, "z%d" % half) for half in range(2)]
+
+        y_codes = tile([P, V], I32, "y_codes")
+        y_scales = tile([P, V], U8, "y_scales")
+        for half in range(2):
+            cols = slice(half * P, (half + 1) * P)
+            acc = psum.tile([P, PACK, P], F32, name="wide", tag="wide")
+            for t in range(PACK):
+                product(acc[:, t, :], w2_codes, w2_sc, t, zq[half][0], zq[half][1])
+            yb = tile([P, P, PACK], BF16, "y_bf%d" % half)
+            nc.vector.tensor_copy(out=yb[:], in_=acc[:].rearrange("p t c -> p c t"))
+            y = tile([P, PACK, P], F32, "y%d" % half)
+            nc.scalar.copy(out=y[:], in_=acc[:])
+            nc.sync.dma_start(out=out_0.rearrange("(p t) v -> p t v", t=PACK)[:, :, cols], in_=y[:])
+            nc.vector.quantize_mx(
+                out=y_codes[:, cols].bitcast(FP8X4), scales=y_scales[:, cols], in_=yb[:].rearrange("p c t -> p (c t)")
+            )
+        nc.sync.dma_start(out=out_1[0].rearrange("p c r -> p (c r)").bitcast(I32), in_=y_codes[:])
+        for q in range(4):
+            queue = nc.sync if q % 2 == 0 else nc.scalar
+            queue.dma_start(
+                out=out_2[0, 4 * q : 4 * q + 4, :].bitcast(I32), in_=y_scales[32 * q : 32 * q + 4, :].bitcast(I32)
+            )

@@ -85,8 +85,8 @@ def tile_picked_dime_none_po_kernel(
                 out=out,
                 lhsT=w_codes[:, cols].bitcast(FP8X4),
                 lhsT_scale=w_scales[:, cols],
-                rhs=codes[:].bitcast(FP8X4),
-                rhs_scale=scales[:],
+                rhs=codes.bitcast(FP8X4),
+                rhs_scale=scales,
                 start=True,
                 stop=True,
             )
@@ -103,14 +103,14 @@ def tile_picked_dime_none_po_kernel(
             w1_raw0 = load_half(first, w1, 0, "w1_raw0")
             load_scale_rows(nc.scalar, xs_all, x_scales)
             xw_all = load_words(sb, x_words, T, "xw_all")
+            w1_raw1 = load_half(sb, w1, 1, "w1_raw1")
             w1_bf0 = round_dealt(nc.vector.tensor_copy, w1_raw0, "w1_bf0")
-        load_scale_rows(nc.gpsimd, w2s_raw, w2_scales)
+        load_scale_rows(nc.scalar, w2s_raw, w2_scales)
         later = ctx.enter_context(tc.tile_pool(name="later", bufs=1))
-        w1_raw1 = load_half(later, w1, 1, "w1_raw1")
-        w3_raw = [load_half(later, w3, half, "w3_raw%d" % half) for half in range(2)]
-        a_raw = [load_half(later, aT, 0, "a_raw0")]
+        w3_raw = [load_half(later, w3, 0, "w3_raw0")]
         w2w_raw = load_words(later, w2_words, H, "w2w_raw")
-        a_raw.append(load_half(later, aT, 1, "a_raw1"))
+        w3_raw.append(load_half(later, w3, 1, "w3_raw1"))
+        a_raw = [load_half(later, aT, d, "a_raw%d" % d) for d in range(2)]
 
         quantize_dealt(w1_bf0, 0, w1_codes, w1_scales)
         xs = tile([P, S], U8, "xs")
@@ -121,39 +121,17 @@ def tile_picked_dime_none_po_kernel(
         h = []
         for t in range(PACK):
             acc = psum.tile([P, S], F32, name="wide", tag="wide")
-            product(acc[:], w1_codes, w1_scales, t, xw, xs)
+            product(acc[:], w1_codes, w1_scales, t, xw[:], xs[:])
             h.append(tile([P, S], F32, "h%d" % t))
             nc.scalar.activation(out=h[t][:], in_=acc[:], func=SILU)
 
-        w3_codes = tile([P, H], U32, "w3_codes")
-        w3_scales = tile([P, H], U8, "w3_scales")
-        for half in range(2):
-            quantize_dealt(round_dealt(nc.vector.tensor_copy, w3_raw[half], "w3_bf%d" % half), half, w3_codes, w3_scales)
+        w3_bf = tile([P, H, PACK], BF16, "w3_bf")
 
-        def filters(d, copy):
-            grouped = tile([P, V, PACK], BF16, "a_bf%d" % d)
-            copy(
-                out=grouped[:].rearrange("p (c i) j -> p c j i", i=4),
-                in_=a_raw[d][:].rearrange("p j (c i) -> p c j i", i=4),
-            )
-            a_codes, a_scales = quantize(grouped, V, "a%d" % d)
-            f = []
-            for pair in range(2):
-                acc = psum.tile([P, 2, V], F32, name="pair", tag="pair")
-                for u in range(2):
-                    product(acc[:, u, :], w3_codes, w3_scales, 2 * pair + u, a_codes, a_scales)
-                held = tile([P, 2, V], F32, "f%d_%d" % (d, pair))
-                nc.scalar.copy(out=held[:], in_=acc[:])
-                f.extend([held[:, 0, :], held[:, 1, :]])
-            return f
+        def round_w3(copy, half):
+            dealt = w3_bf[:].rearrange("p (t m) j -> p m j t", t=PACK)[:, half * HM : (half + 1) * HM]
+            copy(out=dealt, in_=w3_raw[half][:].rearrange("p j (m t) -> p m j t", t=PACK))
 
-        def messages(d, f):
-            prod = tile([P, PACK, V], F32, "prod%d" % d)
-            for t in range(PACK):
-                nc.vector.tensor_tensor(out=prod[:, t, :], in0=h[t][:].indirect(pos_t[d][:]), in1=f[t], op=MULT)
-            return prod
-
-        f0 = filters(0, nc.vector.tensor_copy)
+        round_w3(nc.vector.tensor_copy, 0)
 
         w2_codes = tile([P, H], I32, "w2_codes")
         nc.vector.tensor_copy(
@@ -164,31 +142,62 @@ def tile_picked_dime_none_po_kernel(
             out=w2_sc[:].rearrange("p (t m) -> p m t", t=PACK), in_=w2s_raw[:].rearrange("p (m t) -> p m t", t=PACK)
         )
 
-        f1 = filters(1, nc.scalar.copy)
-        prods = [messages(0, f0), messages(1, f1)]
+        picked = [tile([P, PACK, V], F32, "picked%d" % d) for d in range(2)]
+        for t in range(PACK):
+            for d in range(2):
+                nc.vector.tensor_copy(out=picked[d][:, t, :], in_=h[t][:].indirect(pos_t[d][:]))
 
-        z = []
+        round_w3(nc.scalar.copy, 1)
+        w3_codes, w3_scales = quantize(w3_bf, H, "w3")
+
+        def filters(d):
+            grouped = tile([P, V, PACK], BF16, "a_bf%d" % d)
+            nc.scalar.copy(
+                out=grouped[:].rearrange("p (c i) j -> p c j i", i=4),
+                in_=a_raw[d][:].rearrange("p j (c i) -> p c j i", i=4),
+            )
+            a_codes, a_scales = quantize(grouped, V, "a%d" % d)
+            banks = []
+            for half in range(2):
+                cols = slice(half * P, (half + 1) * P)
+                acc = psum.tile([P, PACK, P], F32, name="filt", tag="filt")
+                for t in range(PACK):
+                    product(acc[:, t, :], w3_codes, w3_scales, t, a_codes[:, cols], a_scales[:, cols])
+                banks.append(acc)
+            return banks
+
+        def weigh(d, half, bank):
+            prod = tile([P, PACK, P], F32, "prod%d_%d" % (d, half))
+            nc.vector.tensor_tensor(
+                out=prod[:], in0=picked[d][:, :, half * P : (half + 1) * P], in1=bank[:], op=MULT
+            )
+            return prod
+
+        f0 = filters(0)
+        f1 = filters(1)
+
+        first_terms = [weigh(0, half, f0[half]) for half in range(2)]
+        y_codes = tile([P, V], I32, "y_codes")
+        y_scales = tile([P, V], U8, "y_scales")
+        zq = []
         for half in range(2):
-            cols = slice(half * P, (half + 1) * P)
+            second = weigh(1, half, f1[half])
             zb = tile([P, P, PACK], BF16, "z_bf%d" % half)
             nc.vector.tensor_tensor(
                 out=zb[:].rearrange("p (c i) t -> p c t i", i=4),
-                in0=prods[0][:, :, cols].rearrange("p t (c i) -> p c t i", i=4),
-                in1=prods[1][:, :, cols].rearrange("p t (c i) -> p c t i", i=4),
+                in0=first_terms[half][:].rearrange("p t (c i) -> p c t i", i=4),
+                in1=second[:].rearrange("p t (c i) -> p c t i", i=4),
                 op=ADD,
             )
-            z.append(zb)
-        zq = [quantize(z[half], P, "z%d" % half) for half in range(2)]
-
-        y_codes = tile([P, V], I32, "y_codes")
-        y_scales = tile([P, V], U8, "y_scales")
+            zq.append(quantize(zb, P, "z%d" % half))
         for half in range(2):
             cols = slice(half * P, (half + 1) * P)
             acc = psum.tile([P, PACK, P], F32, name="wide", tag="wide")
             for t in range(PACK):
-                product(acc[:, t, :], w2_codes, w2_sc, t, zq[half][0], zq[half][1])
+                product(acc[:, t, :], w2_codes, w2_sc, t, zq[half][0][:], zq[half][1][:])
             yb = tile([P, P, PACK], BF16, "y_bf%d" % half)
-            nc.vector.tensor_copy(out=yb[:], in_=acc[:].rearrange("p t c -> p c t"))
+            copy = nc.scalar.copy if half == 0 else nc.vector.tensor_copy
+            copy(out=yb[:], in_=acc[:].rearrange("p t c -> p c t"))
             y = tile([P, PACK, P], F32, "y%d" % half)
             nc.scalar.copy(out=y[:], in_=acc[:])
             nc.sync.dma_start(out=out_0.rearrange("(p t) v -> p t v", t=PACK)[:, :, cols], in_=y[:])

@@ -29,16 +29,15 @@ def tile_picked_dime_none_po_kernel(
     with ExitStack() as ctx:
         lists = ctx.enter_context(tc.tile_pool(name="lists", bufs=1))
         sb = ctx.enter_context(tc.tile_pool(name="sb", bufs=1))
-        psum = ctx.enter_context(tc.psum_pool(name="psum", bufs=4))
+        psum = ctx.enter_context(tc.psum_pool(name="psum", bufs=8))
 
         def tile(shape, dtype, name):
             return sb.tile(shape, dtype, name=name, align_bytes=64)
 
-        def load_half(pool, src, half, name):
-            raw = pool.tile([P, PACK, HALF], F32, name=name)
-            nc.sync.dma_start(
-                out=raw[:], in_=src.rearrange("(p j) c -> p j c", j=PACK)[:, :, half * HALF : (half + 1) * HALF]
-            )
+        def load_rows(pool, src, cols, name):
+            part = src.rearrange("(p j) c -> p j c", j=PACK)[:, :, cols]
+            raw = pool.tile(list(part.shape), F32, name=name, align_bytes=64)
+            nc.sync.dma_start(out=raw[:], in_=part)
             return raw
 
         def load_scale_rows(queue, plane, src):
@@ -57,19 +56,13 @@ def tile_picked_dime_none_po_kernel(
             nc.sync.dma_start(out=words[:], in_=src[0].rearrange("p c r -> p (c r)").bitcast(I32))
             return words
 
-        def round_dealt(copy, raw, name):
-            dealt = tile([P, PACK, HM, PACK], BF16, name)
-            copy(out=dealt[:].rearrange("p t m j -> p m j t"), in_=raw[:].rearrange("p j (m t) -> p m j t", t=PACK))
-            return dealt
-
-        def quantize_dealt(dealt, half, codes, scales):
-            for t in range(PACK):
-                cols = slice(t * P + half * HM, t * P + (half + 1) * HM)
-                nc.vector.quantize_mx(
-                    out=codes[:, cols].bitcast(FP8X4),
-                    scales=scales[:, cols],
-                    in_=dealt[:, t].rearrange("p m j -> p (m j)"),
-                )
+        def quantize_dealt(raw, split, name):
+            grouped = tile([P, H, PACK], BF16, name + "_bf")
+            dealt = grouped[:].rearrange("p (t m) j -> p m t j", t=PACK)
+            source = raw[:].rearrange("p j (m t) -> p m t j", t=PACK)
+            nc.vector.tensor_copy(out=dealt[:, :split], in_=source[:, :split])
+            nc.scalar.copy(out=dealt[:, split:], in_=source[:, split:])
+            return quantize(grouped, H, name)
 
         def quantize(grouped, columns, name):
             codes = tile([P, columns], U32, name + "_codes")
@@ -91,108 +84,113 @@ def tile_picked_dime_none_po_kernel(
                 stop=True,
             )
 
+        def bank(shape):
+            return psum.tile(shape, F32, name="bank", tag="bank")
+
         xs_all = tile([P, T], U8, "xs_all")
         nc.vector.memset(xs_all[:].bitcast(I32), 0)
         w2s_raw = tile([P, H], U8, "w2s_raw")
         nc.vector.memset(w2s_raw[:].bitcast(I32), 0)
         offs_t = load_list(offs, S, "offs_t")
         pos_t = [load_list(pos1, V, "pos1_t"), load_list(pos2, V, "pos2_t")]
-        w1_codes = tile([P, H], U32, "w1_codes")
-        w1_scales = tile([P, H], U8, "w1_scales")
-        with tc.tile_pool(name="first", bufs=1) as first:
-            w1_raw0 = load_half(first, w1, 0, "w1_raw0")
-            load_scale_rows(nc.scalar, xs_all, x_scales)
-            xw_all = load_words(sb, x_words, T, "xw_all")
-            w1_raw1 = load_half(sb, w1, 1, "w1_raw1")
-            w1_bf0 = round_dealt(nc.vector.tensor_copy, w1_raw0, "w1_bf0")
-        load_scale_rows(nc.scalar, w2s_raw, w2_scales)
-        later = ctx.enter_context(tc.tile_pool(name="later", bufs=1))
-        w3_raw = [load_half(later, w3, 0, "w3_raw0")]
-        w2w_raw = load_words(later, w2_words, H, "w2w_raw")
-        w3_raw.append(load_half(later, w3, 1, "w3_raw1"))
-        a_raw = [load_half(later, aT, d, "a_raw%d" % d) for d in range(2)]
 
-        quantize_dealt(w1_bf0, 0, w1_codes, w1_scales)
-        xs = tile([P, S], U8, "xs")
-        nc.vector.tensor_copy(out=xs[:], in_=xs_all[:].indirect(offs_t[:]))
-        xw = tile([P, S], U32, "xw")
-        nc.vector.tensor_copy(out=xw[:], in_=xw_all[:].bitcast(U32).indirect(offs_t[:]))
-        quantize_dealt(round_dealt(nc.vector.tensor_copy, w1_raw1, "w1_bf1"), 1, w1_codes, w1_scales)
-        h = []
-        for t in range(PACK):
-            acc = psum.tile([P, S], F32, name="wide", tag="wide")
-            product(acc[:], w1_codes, w1_scales, t, xw[:], xs[:])
-            h.append(tile([P, S], F32, "h%d" % t))
-            nc.scalar.activation(out=h[t][:], in_=acc[:], func=SILU)
-
-        w3_bf = tile([P, H, PACK], BF16, "w3_bf")
-
-        def round_w3(copy, half):
-            dealt = w3_bf[:].rearrange("p (t m) j -> p m j t", t=PACK)[:, half * HM : (half + 1) * HM]
-            copy(out=dealt, in_=w3_raw[half][:].rearrange("p j (m t) -> p m j t", t=PACK))
-
-        round_w3(nc.vector.tensor_copy, 0)
-
-        w2_codes = tile([P, H], I32, "w2_codes")
-        nc.vector.tensor_copy(
-            out=w2_codes[:].rearrange("p (t m) -> p m t", t=PACK), in_=w2w_raw[:].rearrange("p (m t) -> p m t", t=PACK)
-        )
-        w2_sc = tile([P, H], U8, "w2_sc")
-        nc.vector.tensor_copy(
-            out=w2_sc[:].rearrange("p (t m) -> p m t", t=PACK), in_=w2s_raw[:].rearrange("p (m t) -> p m t", t=PACK)
-        )
-
-        picked = [tile([P, PACK, V], F32, "picked%d" % d) for d in range(2)]
-        for t in range(PACK):
-            for d in range(2):
-                nc.vector.tensor_copy(out=picked[d][:, t, :], in_=h[t][:].indirect(pos_t[d][:]))
-
-        round_w3(nc.scalar.copy, 1)
-        w3_codes, w3_scales = quantize(w3_bf, H, "w3")
-
-        def filters(d):
-            grouped = tile([P, V, PACK], BF16, "a_bf%d" % d)
-            nc.scalar.copy(
+        def round_angles(raw, name):
+            grouped = tile([P, V, PACK], BF16, name)
+            nc.vector.tensor_copy(
                 out=grouped[:].rearrange("p (c i) j -> p c j i", i=4),
-                in_=a_raw[d][:].rearrange("p j (c i) -> p c j i", i=4),
+                in_=raw[:].rearrange("p j (c i) -> p c j i", i=4),
             )
-            a_codes, a_scales = quantize(grouped, V, "a%d" % d)
+            return grouped
+
+        with tc.tile_pool(name="first", bufs=1) as first:
+            a_raw0 = load_rows(first, aT, slice(0, V), "a_raw0")
+            w3_raw = load_rows(sb, w3, slice(0, H), "w3_raw")
+            load_scale_rows(nc.scalar, xs_all, x_scales)
+            load_scale_rows(nc.scalar, w2s_raw, w2_scales)
+            a_bf0 = round_angles(a_raw0, "a_bf0")
+        later = ctx.enter_context(tc.tile_pool(name="later", bufs=1))
+        w1_raw = load_rows(later, w1, slice(0, H), "w1_raw")
+        xw_all = load_words(later, x_words, T, "xw_all")
+        a_raw1 = load_rows(later, aT, slice(V, 2 * V), "a_raw1")
+        w2w_raw = load_words(later, w2_words, H, "w2w_raw")
+
+        w3_codes, w3_scales = quantize_dealt(w3_raw, 80, "w3")
+
+        def filters(grouped, name):
+            a_codes, a_scales = quantize(grouped, V, name)
             banks = []
-            for half in range(2):
-                cols = slice(half * P, (half + 1) * P)
-                acc = psum.tile([P, PACK, P], F32, name="filt", tag="filt")
-                for t in range(PACK):
-                    product(acc[:, t, :], w3_codes, w3_scales, t, a_codes[:, cols], a_scales[:, cols])
+            for pair in range(2):
+                acc = bank([P, 2, V])
+                for u in range(2):
+                    product(acc[:, u, :], w3_codes, w3_scales, 2 * pair + u, a_codes[:], a_scales[:])
                 banks.append(acc)
             return banks
 
-        def weigh(d, half, bank):
-            prod = tile([P, PACK, P], F32, "prod%d_%d" % (d, half))
-            nc.vector.tensor_tensor(
-                out=prod[:], in0=picked[d][:, :, half * P : (half + 1) * P], in1=bank[:], op=MULT
+        def hold(banks, copies, name):
+            rows = []
+            for pair in range(2):
+                held = tile([P, 2, V], F32, "%s_%d" % (name, pair))
+                copies[pair](out=held[:], in_=banks[pair][:])
+                rows.extend([held[:, 0, :], held[:, 1, :]])
+            return rows
+
+        f0 = hold(filters(a_bf0, "a0"), [nc.scalar.copy, nc.scalar.copy], "f0")
+        xs = tile([P, S], U8, "xs")
+        nc.vector.tensor_copy(out=xs[:], in_=xs_all[:].indirect(offs_t[:]))
+        w1_codes, w1_scales = quantize_dealt(w1_raw, 88, "w1")
+
+        xw = tile([P, S], U32, "xw")
+        for half in range(2):
+            nc.vector.tensor_copy(
+                out=xw[:, half * HALF : (half + 1) * HALF],
+                in_=xw_all[:].bitcast(U32).indirect(offs_t[:, half * HALF // 16 : (half + 1) * HALF // 16]),
             )
-            return prod
+        h = []
+        for t in range(PACK):
+            h.append(tile([P, S], F32, "h%d" % t))
+            width = HALF if t == 0 else S
+            for c0 in range(0, S, width):
+                cols = slice(c0, c0 + width)
+                acc = bank([P, width])
+                product(acc[:], w1_codes, w1_scales, t, xw[:, cols], xs[:, cols])
+                nc.scalar.activation(out=h[t][:, cols], in_=acc[:], func=SILU)
 
-        f0 = filters(0)
-        f1 = filters(1)
+        f1 = hold(filters(round_angles(a_raw1, "a_bf1"), "a1"), [nc.scalar.copy, nc.scalar.copy], "f1")
 
-        first_terms = [weigh(0, half, f0[half]) for half in range(2)]
-        y_codes = tile([P, V], I32, "y_codes")
-        y_scales = tile([P, V], U8, "y_scales")
+        w2_codes = tile([P, H], I32, "w2_codes")
+        nc.vector.tensor_copy(
+            out=w2_codes[:].rearrange("p (t r i) -> p r t i", t=PACK, i=4),
+            in_=w2w_raw[:].rearrange("p (r i t) -> p r t i", t=PACK, i=4),
+        )
+        w2_sc = tile([P, H], U8, "w2_sc")
+        nc.vector.tensor_copy(
+            out=w2_sc[:].rearrange("p (t r i) -> p r t i", t=PACK, i=16),
+            in_=w2s_raw[:].rearrange("p (r i t) -> p r t i", t=PACK, i=16),
+        )
+
+        terms = []
+        for d, f in enumerate((f0, f1)):
+            terms.append(tile([P, PACK, V], F32, "terms%d" % d))
+            for t in range(PACK):
+                nc.vector.tensor_tensor(out=terms[d][:, t, :], in0=h[t][:].indirect(pos_t[d][:]), in1=f[t], op=MULT)
+        first_terms, second_terms = terms
+
         zq = []
         for half in range(2):
-            second = weigh(1, half, f1[half])
+            cols = slice(half * P, (half + 1) * P)
             zb = tile([P, P, PACK], BF16, "z_bf%d" % half)
             nc.vector.tensor_tensor(
                 out=zb[:].rearrange("p (c i) t -> p c t i", i=4),
-                in0=first_terms[half][:].rearrange("p t (c i) -> p c t i", i=4),
-                in1=second[:].rearrange("p t (c i) -> p c t i", i=4),
+                in0=first_terms[:, :, cols].rearrange("p t (c i) -> p c t i", i=4),
+                in1=second_terms[:, :, cols].rearrange("p t (c i) -> p c t i", i=4),
                 op=ADD,
             )
             zq.append(quantize(zb, P, "z%d" % half))
+        y_codes = tile([P, V], I32, "y_codes")
+        y_scales = tile([P, V], U8, "y_scales")
         for half in range(2):
             cols = slice(half * P, (half + 1) * P)
-            acc = psum.tile([P, PACK, P], F32, name="wide", tag="wide")
+            acc = bank([P, PACK, P])
             for t in range(PACK):
                 product(acc[:, t, :], w2_codes, w2_sc, t, zq[half][0][:], zq[half][1][:])
             yb = tile([P, P, PACK], BF16, "y_bf%d" % half)

@@ -91,6 +91,7 @@ def tile_picked_dime_none_po_kernel(
         nc.vector.memset(xs_all[:].bitcast(I32), 0)
         w2s_raw = tile([P, H], U8, "w2s_raw")
         nc.vector.memset(w2s_raw[:].bitcast(I32), 0)
+
         offs_t = load_list(offs, S, "offs_t")
         pos_t = [load_list(pos1, V, "pos1_t"), load_list(pos2, V, "pos2_t")]
 
@@ -178,12 +179,13 @@ def tile_picked_dime_none_po_kernel(
         zq = []
         for half in range(2):
             cols = slice(half * P, (half + 1) * P)
+            summed = tile([P, PACK, P], BF16, "z_rows%d" % half)
+            nc.vector.tensor_tensor(out=summed[:], in0=first_terms[:, :, cols], in1=second_terms[:, :, cols], op=ADD)
             zb = tile([P, P, PACK], BF16, "z_bf%d" % half)
-            nc.vector.tensor_tensor(
+            weave = nc.scalar.copy if half == 0 else nc.vector.tensor_copy
+            weave(
                 out=zb[:].rearrange("p (c i) t -> p c t i", i=4),
-                in0=first_terms[:, :, cols].rearrange("p t (c i) -> p c t i", i=4),
-                in1=second_terms[:, :, cols].rearrange("p t (c i) -> p c t i", i=4),
-                op=ADD,
+                in_=summed[:].rearrange("p t (c i) -> p c t i", i=4),
             )
             zq.append(quantize(zb, P, "z%d" % half))
         y_codes = tile([P, V], I32, "y_codes")

@@ -19,7 +19,6 @@ SILU = mybir.ActivationFunctionType.Silu
 P = 128
 PACK = 4
 HALF = 256
-HM = HALF // PACK
 
 
 def tile_picked_dime_none_po_kernel(
@@ -31,19 +30,19 @@ def tile_picked_dime_none_po_kernel(
         sb = ctx.enter_context(tc.tile_pool(name="sb", bufs=1))
         psum = ctx.enter_context(tc.psum_pool(name="psum", bufs=8))
 
-        def tile(shape, dtype, name):
-            return sb.tile(shape, dtype, name=name, align_bytes=64)
+        def tile(shape, dtype, name, pool=sb):
+            return pool.tile(shape, dtype, name=name, align_bytes=64)
 
         def load_rows(pool, src, cols, name):
             part = src.rearrange("(p j) c -> p j c", j=PACK)[:, :, cols]
-            raw = pool.tile(list(part.shape), F32, name=name, align_bytes=64)
+            raw = tile(list(part.shape), F32, name, pool)
             nc.sync.dma_start(out=raw[:], in_=part)
             return raw
 
-        def load_scale_rows(queue, plane, src):
+        def place_scale_rows(plane, rows):
             for q in range(4):
-                queue.dma_start(
-                    out=plane[32 * q : 32 * q + 4, :].bitcast(I32), in_=src[0, 4 * q : 4 * q + 4, :].bitcast(I32)
+                nc.sync.dma_start(
+                    out=plane[32 * q : 32 * q + 4, :].bitcast(I32), in_=rows[4 * q : 4 * q + 4, :].bitcast(I32)
                 )
 
         def load_list(src, entries, name):
@@ -52,17 +51,18 @@ def tile_picked_dime_none_po_kernel(
             return held
 
         def load_words(pool, src, columns, name):
-            words = pool.tile([P, columns], I32, name=name, align_bytes=64)
+            words = tile([P, columns], I32, name, pool)
             nc.sync.dma_start(out=words[:], in_=src[0].rearrange("p c r -> p (c r)").bitcast(I32))
             return words
 
-        def quantize_dealt(raw, split, name):
+        def round_dealt(raw, split, name):
             grouped = tile([P, H, PACK], BF16, name + "_bf")
             dealt = grouped[:].rearrange("p (t m) j -> p m t j", t=PACK)
             source = raw[:].rearrange("p j (m t) -> p m t j", t=PACK)
-            nc.vector.tensor_copy(out=dealt[:, :split], in_=source[:, :split])
+            if split > 0:
+                nc.vector.tensor_copy(out=dealt[:, :split], in_=source[:, :split])
             nc.scalar.copy(out=dealt[:, split:], in_=source[:, split:])
-            return quantize(grouped, H, name)
+            return grouped
 
         def quantize(grouped, columns, name):
             codes = tile([P, columns], U32, name + "_codes")
@@ -87,58 +87,61 @@ def tile_picked_dime_none_po_kernel(
         def bank(shape):
             return psum.tile(shape, F32, name="bank", tag="bank")
 
-        xs_all = tile([P, T], U8, "xs_all")
-        nc.vector.memset(xs_all[:].bitcast(I32), 0)
-        w2s_raw = tile([P, H], U8, "w2s_raw")
-        nc.vector.memset(w2s_raw[:].bitcast(I32), 0)
+        warm_in = tile([P, 1], F32, "warm_in")
+        nc.gpsimd.memset(warm_in[:], 0.0)
+        warm_out = tile([P, 1], F32, "warm_out")
+        nc.scalar.activation(out=warm_out[:], in_=warm_in[:], func=SILU)
 
-        offs_t = load_list(offs, S, "offs_t")
-        pos_t = [load_list(pos1, V, "pos1_t"), load_list(pos2, V, "pos2_t")]
-
-        def round_angles(raw, name):
-            grouped = tile([P, V, PACK], BF16, name)
+        with tc.tile_pool(name="first", bufs=1) as first:
+            xs_all = tile([P, T], U8, "xs_all", first)
+            nc.vector.memset(xs_all[:].bitcast(I32), 0)
+            w2s_raw = tile([P, H], U8, "w2s_raw")
+            nc.vector.memset(w2s_raw[:].bitcast(I32), 0)
+            xs = tile([P, S], U8, "xs")
+            nc.vector.memset(xs[:].bitcast(I32), 0)
+            offs_t = load_list(offs, S, "offs_t")
+            a_raw0 = load_rows(sb, aT, slice(0, V), "a_raw0")
+            nc.sync.dma_start(out=xs_all[0:16, :].bitcast(I32), in_=x_scales[0].bitcast(I32))
+            pos_t = [load_list(pos1, V, "pos1_t"), load_list(pos2, V, "pos2_t")]
+            nc.sync.dma_start(out=w2s_raw[0:16, :].bitcast(I32), in_=w2_scales[0].bitcast(I32))
+            w3_raw = load_rows(sb, w3, slice(0, H), "w3_raw")
+            w1_raw = load_rows(sb, w1, slice(0, H), "w1_raw")
+            xs_rows = tile([P, S], U8, "xs_rows")
+            nc.vector.tensor_copy(out=xs_rows[:], in_=xs_all[:].indirect(offs_t[:]))
+            place_scale_rows(xs, xs_rows)
+            w2s_dealt = tile([P, H], U8, "w2s_dealt")
             nc.vector.tensor_copy(
+                out=w2s_dealt[:].rearrange("p (t r i) -> p r t i", t=PACK, i=16),
+                in_=w2s_raw[:].rearrange("p (r i t) -> p r t i", t=PACK, i=16),
+            )
+        later = ctx.enter_context(tc.tile_pool(name="later", bufs=1))
+        xw_all = load_words(later, x_words, T, "xw_all")
+        a_raw1 = load_rows(later, aT, slice(V, 2 * V), "a_raw1")
+        w2w_raw = load_words(later, w2_words, H, "w2w_raw")
+        w2_sc = tile([P, H], U8, "w2_sc", later)
+        nc.vector.memset(w2_sc[:].bitcast(I32), 0)
+        place_scale_rows(w2_sc, w2s_dealt)
+
+        def round_angles(copy, raw, name):
+            grouped = tile([P, V, PACK], BF16, name)
+            copy(
                 out=grouped[:].rearrange("p (c i) j -> p c j i", i=4),
                 in_=raw[:].rearrange("p j (c i) -> p c j i", i=4),
             )
             return grouped
 
-        with tc.tile_pool(name="first", bufs=1) as first:
-            a_raw0 = load_rows(first, aT, slice(0, V), "a_raw0")
-            w3_raw = load_rows(sb, w3, slice(0, H), "w3_raw")
-            load_scale_rows(nc.scalar, xs_all, x_scales)
-            load_scale_rows(nc.scalar, w2s_raw, w2_scales)
-            a_bf0 = round_angles(a_raw0, "a_bf0")
-        later = ctx.enter_context(tc.tile_pool(name="later", bufs=1))
-        w1_raw = load_rows(later, w1, slice(0, H), "w1_raw")
-        xw_all = load_words(later, x_words, T, "xw_all")
-        a_raw1 = load_rows(later, aT, slice(V, 2 * V), "a_raw1")
-        w2w_raw = load_words(later, w2_words, H, "w2w_raw")
-
-        w3_codes, w3_scales = quantize_dealt(w3_raw, 80, "w3")
-
-        def filters(grouped, name):
-            a_codes, a_scales = quantize(grouped, V, name)
-            banks = []
+        def filters(a_codes, a_scales, held):
             for pair in range(2):
                 acc = bank([P, 2, V])
                 for u in range(2):
                     product(acc[:, u, :], w3_codes, w3_scales, 2 * pair + u, a_codes[:], a_scales[:])
-                banks.append(acc)
-            return banks
+                nc.scalar.copy(out=held[:, 2 * pair : 2 * pair + 2, :], in_=acc[:])
+            return held
 
-        def hold(banks, copies, name):
-            rows = []
-            for pair in range(2):
-                held = tile([P, 2, V], F32, "%s_%d" % (name, pair))
-                copies[pair](out=held[:], in_=banks[pair][:])
-                rows.extend([held[:, 0, :], held[:, 1, :]])
-            return rows
-
-        f0 = hold(filters(a_bf0, "a0"), [nc.scalar.copy, nc.scalar.copy], "f0")
-        xs = tile([P, S], U8, "xs")
-        nc.vector.tensor_copy(out=xs[:], in_=xs_all[:].indirect(offs_t[:]))
-        w1_codes, w1_scales = quantize_dealt(w1_raw, 88, "w1")
+        a0_codes, a0_scales = quantize(round_angles(nc.scalar.copy, a_raw0, "a_bf0"), V, "a0")
+        w3_codes, w3_scales = quantize(round_dealt(w3_raw, 84, "w3"), H, "w3")
+        w1_codes, w1_scales = quantize(round_dealt(w1_raw, 84, "w1"), H, "w1")
+        f0 = filters(a0_codes, a0_scales, sb.tile([P, PACK, V], F32, name="f0", tag="w1_raw", align_bytes=64))
 
         xw = tile([P, S], U32, "xw")
         for half in range(2):
@@ -156,55 +159,55 @@ def tile_picked_dime_none_po_kernel(
                 product(acc[:], w1_codes, w1_scales, t, xw[:, cols], xs[:, cols])
                 nc.scalar.activation(out=h[t][:, cols], in_=acc[:], func=SILU)
 
-        f1 = hold(filters(round_angles(a_raw1, "a_bf1"), "a1"), [nc.scalar.copy, nc.scalar.copy], "f1")
-
-        w2_codes = tile([P, H], I32, "w2_codes")
-        nc.vector.tensor_copy(
-            out=w2_codes[:].rearrange("p (t r i) -> p r t i", t=PACK, i=4),
-            in_=w2w_raw[:].rearrange("p (r i t) -> p r t i", t=PACK, i=4),
-        )
-        w2_sc = tile([P, H], U8, "w2_sc")
-        nc.vector.tensor_copy(
-            out=w2_sc[:].rearrange("p (t r i) -> p r t i", t=PACK, i=16),
-            in_=w2s_raw[:].rearrange("p (r i t) -> p r t i", t=PACK, i=16),
-        )
+        a1_codes, a1_scales = quantize(round_angles(nc.vector.tensor_copy, a_raw1, "a_bf1"), V, "a1")
+        f1 = filters(a1_codes, a1_scales, tile([P, PACK, V], F32, "f1"))
 
         terms = []
         for d, f in enumerate((f0, f1)):
             terms.append(tile([P, PACK, V], F32, "terms%d" % d))
             for t in range(PACK):
-                nc.vector.tensor_tensor(out=terms[d][:, t, :], in0=h[t][:].indirect(pos_t[d][:]), in1=f[t], op=MULT)
+                nc.vector.tensor_tensor(out=terms[d][:, t, :], in0=h[t][:].indirect(pos_t[d][:]), in1=f[:, t, :], op=MULT)
         first_terms, second_terms = terms
 
-        zq = []
-        for half in range(2):
+        def add_terms(half):
             cols = slice(half * P, (half + 1) * P)
-            summed = tile([P, PACK, P], BF16, "z_rows%d" % half)
-            nc.vector.tensor_tensor(out=summed[:], in0=first_terms[:, :, cols], in1=second_terms[:, :, cols], op=ADD)
             zb = tile([P, P, PACK], BF16, "z_bf%d" % half)
-            weave = nc.scalar.copy if half == 0 else nc.vector.tensor_copy
-            weave(
+            nc.vector.tensor_tensor(
                 out=zb[:].rearrange("p (c i) t -> p c t i", i=4),
-                in_=summed[:].rearrange("p t (c i) -> p c t i", i=4),
+                in0=first_terms[:, :, cols].rearrange("p t (c i) -> p c t i", i=4),
+                in1=second_terms[:, :, cols].rearrange("p t (c i) -> p c t i", i=4),
+                op=ADD,
             )
-            zq.append(quantize(zb, P, "z%d" % half))
+            return zb
+
+        zb0 = add_terms(0)
+        w2_codes = sb.tile([P, H], I32, name="w2_codes", tag="h3", align_bytes=64)
+        nc.vector.tensor_copy(
+            out=w2_codes[:].rearrange("p (t r i) -> p r t i", t=PACK, i=4),
+            in_=w2w_raw[:].rearrange("p (r i t) -> p r t i", t=PACK, i=4),
+        )
+        zq = [quantize(zb0, P, "z0"), quantize(add_terms(1), P, "z1")]
+
         y_codes = tile([P, V], I32, "y_codes")
         y_scales = tile([P, V], U8, "y_scales")
+        words_out = out_1[0].rearrange("p c r -> p (c r)").bitcast(I32)
         for half in range(2):
             cols = slice(half * P, (half + 1) * P)
-            acc = bank([P, PACK, P])
-            for t in range(PACK):
-                product(acc[:, t, :], w2_codes, w2_sc, t, zq[half][0][:], zq[half][1][:])
-            yb = tile([P, P, PACK], BF16, "y_bf%d" % half)
-            copy = nc.scalar.copy if half == 0 else nc.vector.tensor_copy
-            copy(out=yb[:], in_=acc[:].rearrange("p t c -> p c t"))
             y = tile([P, PACK, P], F32, "y%d" % half)
-            nc.scalar.copy(out=y[:], in_=acc[:])
+            for pair in range(2):
+                acc = bank([P, 2, P])
+                for u in range(2):
+                    product(acc[:, u, :], w2_codes, w2_sc, 2 * pair + u, zq[half][0][:], zq[half][1][:])
+                nc.scalar.copy(out=y[:, 2 * pair : 2 * pair + 2, :], in_=acc[:])
             nc.sync.dma_start(out=out_0.rearrange("(p t) v -> p t v", t=PACK)[:, :, cols], in_=y[:])
+            yb = tile([P, P, PACK], BF16, "y_bf%d" % half)
+            nc.vector.tensor_copy(
+                out=yb[:].rearrange("p (c i) t -> p c t i", i=4), in_=y[:].rearrange("p t (c i) -> p c t i", i=4)
+            )
             nc.vector.quantize_mx(
                 out=y_codes[:, cols].bitcast(FP8X4), scales=y_scales[:, cols], in_=yb[:].rearrange("p c t -> p (c t)")
             )
-        nc.sync.dma_start(out=out_1[0].rearrange("p c r -> p (c r)").bitcast(I32), in_=y_codes[:])
+            nc.sync.dma_start(out=words_out[:, cols], in_=y_codes[:, cols])
         for q in range(4):
             queue = nc.sync if q % 2 == 0 else nc.scalar
             queue.dma_start(

@@ -39,9 +39,9 @@ def tile_picked_dime_none_po_kernel(
             nc.sync.dma_start(out=raw[:], in_=part)
             return raw
 
-        def place_scale_rows(plane, rows):
+        def place_scale_rows(queue, plane, rows):
             for q in range(4):
-                nc.sync.dma_start(
+                queue.dma_start(
                     out=plane[32 * q : 32 * q + 4, :].bitcast(I32), in_=rows[4 * q : 4 * q + 4, :].bitcast(I32)
                 )
 
@@ -99,36 +99,33 @@ def tile_picked_dime_none_po_kernel(
             nc.vector.memset(w2s_raw[:].bitcast(I32), 0)
             xs = tile([P, S], U8, "xs")
             nc.vector.memset(xs[:].bitcast(I32), 0)
-            offs_t = load_list(offs, S, "offs_t")
             a_raw0 = load_rows(sb, aT, slice(0, V), "a_raw0")
+            offs_t = load_list(offs, S, "offs_t")
             nc.sync.dma_start(out=xs_all[0:16, :].bitcast(I32), in_=x_scales[0].bitcast(I32))
             pos_t = [load_list(pos1, V, "pos1_t"), load_list(pos2, V, "pos2_t")]
             nc.sync.dma_start(out=w2s_raw[0:16, :].bitcast(I32), in_=w2_scales[0].bitcast(I32))
             w3_raw = load_rows(sb, w3, slice(0, H), "w3_raw")
             w1_raw = load_rows(sb, w1, slice(0, H), "w1_raw")
+            xw_all = load_words(sb, x_words, T, "xw_all")
             xs_rows = tile([P, S], U8, "xs_rows")
             nc.vector.tensor_copy(out=xs_rows[:], in_=xs_all[:].indirect(offs_t[:]))
-            place_scale_rows(xs, xs_rows)
+            place_scale_rows(nc.scalar, xs, xs_rows)
             w2s_dealt = tile([P, H], U8, "w2s_dealt")
             nc.vector.tensor_copy(
                 out=w2s_dealt[:].rearrange("p (t r i) -> p r t i", t=PACK, i=16),
                 in_=w2s_raw[:].rearrange("p (r i t) -> p r t i", t=PACK, i=16),
             )
         later = ctx.enter_context(tc.tile_pool(name="later", bufs=1))
-        xw_all = load_words(later, x_words, T, "xw_all")
-        a_raw1 = load_rows(later, aT, slice(V, 2 * V), "a_raw1")
+        a_raw1 = [load_rows(later, aT, slice(V + s * P, V + (s + 1) * P), "a_raw1_%d" % s) for s in range(2)]
         w2w_raw = load_words(later, w2_words, H, "w2w_raw")
         w2_sc = tile([P, H], U8, "w2_sc", later)
         nc.vector.memset(w2_sc[:].bitcast(I32), 0)
-        place_scale_rows(w2_sc, w2s_dealt)
+        place_scale_rows(nc.sync, w2_sc, w2s_dealt)
 
-        def round_angles(copy, raw, name):
-            grouped = tile([P, V, PACK], BF16, name)
+        def round_angles(copy, out, raw):
             copy(
-                out=grouped[:].rearrange("p (c i) j -> p c j i", i=4),
-                in_=raw[:].rearrange("p j (c i) -> p c j i", i=4),
+                out=out.rearrange("p (c i) j -> p c j i", i=4), in_=raw[:].rearrange("p j (c i) -> p c j i", i=4)
             )
-            return grouped
 
         def filters(a_codes, a_scales, held):
             for pair in range(2):
@@ -138,7 +135,9 @@ def tile_picked_dime_none_po_kernel(
                 nc.scalar.copy(out=held[:, 2 * pair : 2 * pair + 2, :], in_=acc[:])
             return held
 
-        a0_codes, a0_scales = quantize(round_angles(nc.scalar.copy, a_raw0, "a_bf0"), V, "a0")
+        a_bf0 = tile([P, V, PACK], BF16, "a_bf0")
+        round_angles(nc.scalar.copy, a_bf0[:], a_raw0)
+        a0_codes, a0_scales = quantize(a_bf0, V, "a0")
         w3_codes, w3_scales = quantize(round_dealt(w3_raw, 84, "w3"), H, "w3")
         w1_codes, w1_scales = quantize(round_dealt(w1_raw, 84, "w1"), H, "w1")
         f0 = filters(a0_codes, a0_scales, sb.tile([P, PACK, V], F32, name="f0", tag="w1_raw", align_bytes=64))
@@ -149,17 +148,20 @@ def tile_picked_dime_none_po_kernel(
                 out=xw[:, half * HALF : (half + 1) * HALF],
                 in_=xw_all[:].bitcast(U32).indirect(offs_t[:, half * HALF // 16 : (half + 1) * HALF // 16]),
             )
+        a_bf1 = tile([P, V, PACK], BF16, "a_bf1")
+        round_angles(nc.scalar.copy, a_bf1[:, :P, :], a_raw1[0])
+        round_angles(nc.vector.tensor_copy, a_bf1[:, P:, :], a_raw1[1])
         h = []
         for t in range(PACK):
             h.append(tile([P, S], F32, "h%d" % t))
-            width = HALF if t == 0 else S
-            for c0 in range(0, S, width):
-                cols = slice(c0, c0 + width)
-                acc = bank([P, width])
+            edges = (0, HALF, HALF + P, S) if t == 0 else (0, S)
+            for c0, c1 in zip(edges[:-1], edges[1:]):
+                cols = slice(c0, c1)
+                acc = bank([P, c1 - c0])
                 product(acc[:], w1_codes, w1_scales, t, xw[:, cols], xs[:, cols])
                 nc.scalar.activation(out=h[t][:, cols], in_=acc[:], func=SILU)
 
-        a1_codes, a1_scales = quantize(round_angles(nc.vector.tensor_copy, a_raw1, "a_bf1"), V, "a1")
+        a1_codes, a1_scales = quantize(a_bf1, V, "a1")
         f1 = filters(a1_codes, a1_scales, tile([P, PACK, V], F32, "f1"))
 
         terms = []

@@ -18,7 +18,14 @@ SILU = mybir.ActivationFunctionType.Silu
 
 P = 128
 PACK = 4
-HALF = 256
+BLOCKS = 16
+QUADRANT = 32
+STRIPE = 16
+PSUM_BANKS = 8
+WORD_GATHER = S // 2
+LINE_WORDS = 4
+LINE_BYTES = 16
+VECTOR_GROUPS = 84
 
 
 def tile_picked_dime_none_po_kernel(
@@ -28,10 +35,16 @@ def tile_picked_dime_none_po_kernel(
     with ExitStack() as ctx:
         lists = ctx.enter_context(tc.tile_pool(name="lists", bufs=1))
         sb = ctx.enter_context(tc.tile_pool(name="sb", bufs=1))
-        psum = ctx.enter_context(tc.psum_pool(name="psum", bufs=8))
+        psum = ctx.enter_context(tc.psum_pool(name="psum", bufs=PSUM_BANKS))
 
         def tile(shape, dtype, name, pool=sb):
             return pool.tile(shape, dtype, name=name, align_bytes=64)
+
+        def tile_over(earlier, shape, dtype, name):
+            return sb.tile(shape, dtype, name=name, tag=earlier, align_bytes=64)
+
+        def bank(shape):
+            return psum.tile(shape, F32, name="bank", tag="bank")
 
         def load_rows(pool, src, cols, name):
             part = src.rearrange("(p j) c -> p j c", j=PACK)[:, :, cols]
@@ -39,14 +52,8 @@ def tile_picked_dime_none_po_kernel(
             nc.sync.dma_start(out=raw[:], in_=part)
             return raw
 
-        def place_scale_rows(queue, plane, rows):
-            for q in range(4):
-                queue.dma_start(
-                    out=plane[32 * q : 32 * q + 4, :].bitcast(I32), in_=rows[4 * q : 4 * q + 4, :].bitcast(I32)
-                )
-
         def load_list(src, entries, name):
-            held = lists.tile([P, entries // 16], U16, name=name)
+            held = lists.tile([P, entries // STRIPE], U16, name=name)
             nc.sync.dma_start(held[:], src)
             return held
 
@@ -55,37 +62,63 @@ def tile_picked_dime_none_po_kernel(
             nc.sync.dma_start(out=words[:], in_=src[0].rearrange("p c r -> p (c r)").bitcast(I32))
             return words
 
-        def round_dealt(raw, split, name):
+        def load_scale_rows(rows, src):
+            nc.sync.dma_start(out=rows[0:BLOCKS, :].bitcast(I32), in_=src[0].bitcast(I32))
+
+        def place_scale_rows(queue, scales, rows):
+            for q in range(BLOCKS // PACK):
+                queue.dma_start(
+                    out=scales[QUADRANT * q : QUADRANT * q + PACK, :].bitcast(I32),
+                    in_=rows[PACK * q : PACK * (q + 1), :].bitcast(I32),
+                )
+
+        def round_dealt(raw, name):
             grouped = tile([P, H, PACK], BF16, name + "_bf")
             dealt = grouped[:].rearrange("p (t m) j -> p m t j", t=PACK)
             source = raw[:].rearrange("p j (m t) -> p m t j", t=PACK)
-            if split > 0:
-                nc.vector.tensor_copy(out=dealt[:, :split], in_=source[:, :split])
-            nc.scalar.copy(out=dealt[:, split:], in_=source[:, split:])
+            nc.vector.tensor_copy(out=dealt[:, :VECTOR_GROUPS], in_=source[:, :VECTOR_GROUPS])
+            nc.scalar.copy(out=dealt[:, VECTOR_GROUPS:], in_=source[:, VECTOR_GROUPS:])
             return grouped
+
+        def by_lines(rows):
+            return rows.rearrange("p j (c i) -> p c j i", i=LINE_WORDS)
+
+        def woven(grouped):
+            return grouped.rearrange("p (c i) j -> p c j i", i=LINE_WORDS)
+
+        def deal(out, raw, run):
+            nc.vector.tensor_copy(
+                out=out[:].rearrange("p (t r i) -> p r t i", t=PACK, i=run),
+                in_=raw[:].rearrange("p (r i t) -> p r t i", t=PACK, i=run),
+            )
+
+        def quantize_into(codes, scales, grouped):
+            nc.vector.quantize_mx(out=codes.bitcast(FP8X4), scales=scales, in_=grouped.rearrange("p c j -> p (c j)"))
 
         def quantize(grouped, columns, name):
             codes = tile([P, columns], U32, name + "_codes")
             scales = tile([P, columns], U8, name + "_scales")
-            nc.vector.quantize_mx(
-                out=codes[:].bitcast(FP8X4), scales=scales[:], in_=grouped[:].rearrange("p c j -> p (c j)")
-            )
+            quantize_into(codes[:], scales[:], grouped[:])
             return codes, scales
 
         def product(out, w_codes, w_scales, t, codes, scales):
-            cols = slice(t * P, (t + 1) * P)
+            places = slice(t * P, (t + 1) * P)
             nc.tensor.matmul_mx(
                 out=out,
-                lhsT=w_codes[:, cols].bitcast(FP8X4),
-                lhsT_scale=w_scales[:, cols],
+                lhsT=w_codes[:, places].bitcast(FP8X4),
+                lhsT_scale=w_scales[:, places],
                 rhs=codes.bitcast(FP8X4),
                 rhs_scale=scales,
                 start=True,
                 stop=True,
             )
 
-        def bank(shape):
-            return psum.tile(shape, F32, name="bank", tag="bank")
+        def products_to_sbuf(held, w_codes, w_scales, codes, scales):
+            for pair in range(PACK // 2):
+                acc = bank([P, 2, held.shape[2]])
+                for u in range(2):
+                    product(acc[:, u, :], w_codes, w_scales, 2 * pair + u, codes, scales)
+                nc.scalar.copy(out=held[:, 2 * pair : 2 * pair + 2, :], in_=acc[:])
 
         warm_in = tile([P, 1], F32, "warm_in")
         nc.gpsimd.memset(warm_in[:], 0.0)
@@ -101,20 +134,19 @@ def tile_picked_dime_none_po_kernel(
             nc.vector.memset(xs[:].bitcast(I32), 0)
             a_raw0 = load_rows(sb, aT, slice(0, V), "a_raw0")
             offs_t = load_list(offs, S, "offs_t")
-            nc.sync.dma_start(out=xs_all[0:16, :].bitcast(I32), in_=x_scales[0].bitcast(I32))
+            load_scale_rows(xs_all, x_scales)
             pos_t = [load_list(pos1, V, "pos1_t"), load_list(pos2, V, "pos2_t")]
-            nc.sync.dma_start(out=w2s_raw[0:16, :].bitcast(I32), in_=w2_scales[0].bitcast(I32))
+            load_scale_rows(w2s_raw, w2_scales)
             w3_raw = load_rows(sb, w3, slice(0, H), "w3_raw")
             w1_raw = load_rows(sb, w1, slice(0, H), "w1_raw")
             xw_all = load_words(sb, x_words, T, "xw_all")
+
             xs_rows = tile([P, S], U8, "xs_rows")
             nc.vector.tensor_copy(out=xs_rows[:], in_=xs_all[:].indirect(offs_t[:]))
             place_scale_rows(nc.scalar, xs, xs_rows)
             w2s_dealt = tile([P, H], U8, "w2s_dealt")
-            nc.vector.tensor_copy(
-                out=w2s_dealt[:].rearrange("p (t r i) -> p r t i", t=PACK, i=16),
-                in_=w2s_raw[:].rearrange("p (r i t) -> p r t i", t=PACK, i=16),
-            )
+            deal(w2s_dealt, w2s_raw, LINE_BYTES)
+
         later = ctx.enter_context(tc.tile_pool(name="later", bufs=1))
         a_raw1 = [load_rows(later, aT, slice(V + s * P, V + (s + 1) * P), "a_raw1_%d" % s) for s in range(2)]
         w2w_raw = load_words(later, w2_words, H, "w2w_raw")
@@ -122,96 +154,78 @@ def tile_picked_dime_none_po_kernel(
         nc.vector.memset(w2_sc[:].bitcast(I32), 0)
         place_scale_rows(nc.sync, w2_sc, w2s_dealt)
 
-        def round_angles(copy, out, raw):
-            copy(
-                out=out.rearrange("p (c i) j -> p c j i", i=4), in_=raw[:].rearrange("p j (c i) -> p c j i", i=4)
-            )
-
-        def filters(a_codes, a_scales, held):
-            for pair in range(2):
-                acc = bank([P, 2, V])
-                for u in range(2):
-                    product(acc[:, u, :], w3_codes, w3_scales, 2 * pair + u, a_codes[:], a_scales[:])
-                nc.scalar.copy(out=held[:, 2 * pair : 2 * pair + 2, :], in_=acc[:])
-            return held
-
         a_bf0 = tile([P, V, PACK], BF16, "a_bf0")
-        round_angles(nc.scalar.copy, a_bf0[:], a_raw0)
+        nc.scalar.copy(out=woven(a_bf0[:]), in_=by_lines(a_raw0[:]))
         a0_codes, a0_scales = quantize(a_bf0, V, "a0")
-        w3_codes, w3_scales = quantize(round_dealt(w3_raw, 84, "w3"), H, "w3")
-        w1_codes, w1_scales = quantize(round_dealt(w1_raw, 84, "w1"), H, "w1")
-        f0 = filters(a0_codes, a0_scales, sb.tile([P, PACK, V], F32, name="f0", tag="w1_raw", align_bytes=64))
+        w3_codes, w3_scales = quantize(round_dealt(w3_raw, "w3"), H, "w3")
+        w1_codes, w1_scales = quantize(round_dealt(w1_raw, "w1"), H, "w1")
+        f0 = tile_over("w1_raw", [P, PACK, V], F32, "f0")
+        products_to_sbuf(f0, w3_codes, w3_scales, a0_codes[:], a0_scales[:])
 
         xw = tile([P, S], U32, "xw")
-        for half in range(2):
+        for c0 in range(0, S, WORD_GATHER):
             nc.vector.tensor_copy(
-                out=xw[:, half * HALF : (half + 1) * HALF],
-                in_=xw_all[:].bitcast(U32).indirect(offs_t[:, half * HALF // 16 : (half + 1) * HALF // 16]),
+                out=xw[:, c0 : c0 + WORD_GATHER],
+                in_=xw_all[:].bitcast(U32).indirect(offs_t[:, c0 // STRIPE : (c0 + WORD_GATHER) // STRIPE]),
             )
         a_bf1 = tile([P, V, PACK], BF16, "a_bf1")
-        round_angles(nc.scalar.copy, a_bf1[:, :P, :], a_raw1[0])
-        round_angles(nc.vector.tensor_copy, a_bf1[:, P:, :], a_raw1[1])
+        nc.scalar.copy(out=woven(a_bf1[:, :P, :]), in_=by_lines(a_raw1[0][:]))
+        nc.vector.tensor_copy(out=woven(a_bf1[:, P:, :]), in_=by_lines(a_raw1[1][:]))
+
         h = []
         for t in range(PACK):
             h.append(tile([P, S], F32, "h%d" % t))
-            edges = (0, HALF, HALF + P, S) if t == 0 else (0, S)
+            edges = (0, WORD_GATHER, WORD_GATHER + P, S) if t == 0 else (0, S)
             for c0, c1 in zip(edges[:-1], edges[1:]):
-                cols = slice(c0, c1)
+                entries = slice(c0, c1)
                 acc = bank([P, c1 - c0])
-                product(acc[:], w1_codes, w1_scales, t, xw[:, cols], xs[:, cols])
-                nc.scalar.activation(out=h[t][:, cols], in_=acc[:], func=SILU)
+                product(acc[:], w1_codes, w1_scales, t, xw[:, entries], xs[:, entries])
+                nc.scalar.activation(out=h[t][:, entries], in_=acc[:], func=SILU)
 
         a1_codes, a1_scales = quantize(a_bf1, V, "a1")
-        f1 = filters(a1_codes, a1_scales, tile([P, PACK, V], F32, "f1"))
+        w2_codes = tile_over("a_bf1", [P, H], I32, "w2_codes")
+        deal(w2_codes, w2w_raw, LINE_WORDS)
+        f1 = tile([P, PACK, V], F32, "f1")
+        products_to_sbuf(f1, w3_codes, w3_scales, a1_codes[:], a1_scales[:])
 
         terms = []
         for d, f in enumerate((f0, f1)):
             terms.append(tile([P, PACK, V], F32, "terms%d" % d))
             for t in range(PACK):
-                nc.vector.tensor_tensor(out=terms[d][:, t, :], in0=h[t][:].indirect(pos_t[d][:]), in1=f[:, t, :], op=MULT)
-        first_terms, second_terms = terms
+                nc.vector.tensor_tensor(
+                    out=terms[d][:, t, :], in0=h[t][:].indirect(pos_t[d][:]), in1=f[:, t, :], op=MULT
+                )
 
-        def add_terms(half):
-            cols = slice(half * P, (half + 1) * P)
-            zb = tile([P, P, PACK], BF16, "z_bf%d" % half)
-            nc.vector.tensor_tensor(
-                out=zb[:].rearrange("p (c i) t -> p c t i", i=4),
-                in0=first_terms[:, :, cols].rearrange("p t (c i) -> p c t i", i=4),
-                in1=second_terms[:, :, cols].rearrange("p t (c i) -> p c t i", i=4),
-                op=ADD,
-            )
-            return zb
-
-        zb0 = add_terms(0)
-        w2_codes = sb.tile([P, H], I32, name="w2_codes", tag="h3", align_bytes=64)
-        nc.vector.tensor_copy(
-            out=w2_codes[:].rearrange("p (t r i) -> p r t i", t=PACK, i=4),
-            in_=w2w_raw[:].rearrange("p (r i t) -> p r t i", t=PACK, i=4),
-        )
-        zq = [quantize(zb0, P, "z0"), quantize(add_terms(1), P, "z1")]
+        zb = tile([P, V, PACK], BF16, "z_bf")
+        z_codes = tile([P, V], U32, "z_codes")
+        z_scales = tile([P, V], U8, "z_scales")
+        for pieces in ((slice(0, P),), (slice(P, P + P // 2), slice(P + P // 2, V))):
+            for targets in pieces:
+                nc.vector.tensor_tensor(
+                    out=woven(zb[:, targets, :]),
+                    in0=by_lines(terms[0][:, :, targets]),
+                    in1=by_lines(terms[1][:, :, targets]),
+                    op=ADD,
+                )
+            for targets in pieces:
+                quantize_into(z_codes[:, targets], z_scales[:, targets], zb[:, targets, :])
 
         y_codes = tile([P, V], I32, "y_codes")
         y_scales = tile([P, V], U8, "y_scales")
+        rows_out = out_0.rearrange("(p t) v -> p t v", t=PACK)
         words_out = out_1[0].rearrange("p c r -> p (c r)").bitcast(I32)
         for half in range(2):
-            cols = slice(half * P, (half + 1) * P)
+            targets = slice(half * P, (half + 1) * P)
             y = tile([P, PACK, P], F32, "y%d" % half)
-            for pair in range(2):
-                acc = bank([P, 2, P])
-                for u in range(2):
-                    product(acc[:, u, :], w2_codes, w2_sc, 2 * pair + u, zq[half][0][:], zq[half][1][:])
-                nc.scalar.copy(out=y[:, 2 * pair : 2 * pair + 2, :], in_=acc[:])
-            nc.sync.dma_start(out=out_0.rearrange("(p t) v -> p t v", t=PACK)[:, :, cols], in_=y[:])
+            products_to_sbuf(y, w2_codes, w2_sc, z_codes[:, targets], z_scales[:, targets])
+            nc.sync.dma_start(out=rows_out[:, :, targets], in_=y[:])
             yb = tile([P, P, PACK], BF16, "y_bf%d" % half)
-            nc.vector.tensor_copy(
-                out=yb[:].rearrange("p (c i) t -> p c t i", i=4), in_=y[:].rearrange("p t (c i) -> p c t i", i=4)
-            )
-            nc.vector.quantize_mx(
-                out=y_codes[:, cols].bitcast(FP8X4), scales=y_scales[:, cols], in_=yb[:].rearrange("p c t -> p (c t)")
-            )
-            nc.sync.dma_start(out=words_out[:, cols], in_=y_codes[:, cols])
-        for q in range(4):
+            nc.vector.tensor_copy(out=woven(yb[:]), in_=by_lines(y[:]))
+            quantize_into(y_codes[:, targets], y_scales[:, targets], yb[:])
+            nc.sync.dma_start(out=words_out[:, targets], in_=y_codes[:, targets])
+        for q in range(BLOCKS // PACK):
             queue = nc.sync if q % 2 == 0 else nc.scalar
             queue.dma_start(
-                out=out_2[0, 4 * q : 4 * q + 4, :].bitcast(I32), in_=y_scales[32 * q : 32 * q + 4, :].bitcast(I32)
+                out=out_2[0, PACK * q : PACK * (q + 1), :].bitcast(I32),
+                in_=y_scales[QUADRANT * q : QUADRANT * q + PACK, :].bitcast(I32),
             )

@@ -192,37 +192,63 @@ def tile_picked_dime_none_po_kernel(
         for d, f in enumerate((f0, f1)):
             terms.append(tile([P, PACK, V], F32, "terms%d" % d))
             for t in range(PACK):
-                nc.vector.tensor_tensor(
-                    out=terms[d][:, t, :], in0=h[t][:].indirect(pos_t[d][:]), in1=f[:, t, :], op=MULT
-                )
+                last = d == 1 and t == PACK - 1
+                for v0, v1 in ((0, P), (P, V)) if last else ((0, V),):
+                    nc.vector.tensor_tensor(
+                        out=terms[d][:, t, v0:v1],
+                        in0=h[t][:].indirect(pos_t[d][:, v0 // STRIPE : v1 // STRIPE]),
+                        in1=f[:, t, v0:v1],
+                        op=MULT,
+                    )
 
         zb = tile([P, V, PACK], BF16, "z_bf")
         z_codes = tile([P, V], U32, "z_codes")
         z_scales = tile([P, V], U8, "z_scales")
-        for pieces in ((slice(0, P),), (slice(P, P + P // 2), slice(P + P // 2, V))):
-            for targets in pieces:
-                nc.vector.tensor_tensor(
-                    out=woven(zb[:, targets, :]),
-                    in0=by_lines(terms[0][:, :, targets]),
-                    in1=by_lines(terms[1][:, :, targets]),
-                    op=ADD,
-                )
-            for targets in pieces:
-                quantize_into(z_codes[:, targets], z_scales[:, targets], zb[:, targets, :])
+        pieces = (slice(0, P), slice(P, P + P // 2), slice(P + P // 2, V))
+
+        def add_terms(targets):
+            nc.vector.tensor_tensor(
+                out=woven(zb[:, targets, :]),
+                in0=by_lines(terms[0][:, :, targets]),
+                in1=by_lines(terms[1][:, :, targets]),
+                op=ADD,
+            )
+
+        def quantize_z(targets):
+            quantize_into(z_codes[:, targets], z_scales[:, targets], zb[:, targets, :])
+
+        add_terms(pieces[0])
+        add_terms(pieces[1])
+        quantize_z(pieces[0])
+        add_terms(pieces[2])
+        quantize_z(pieces[1])
+        quantize_z(pieces[2])
 
         y_codes = tile([P, V], I32, "y_codes")
         y_scales = tile([P, V], U8, "y_scales")
+        yb = tile([P, V, PACK], BF16, "y_bf")
         rows_out = out_0.rearrange("(p t) v -> p t v", t=PACK)
-        words_out = out_1[0].rearrange("p c r -> p (c r)").bitcast(I32)
-        for half in range(2):
-            targets = slice(half * P, (half + 1) * P)
-            y = tile([P, PACK, P], F32, "y%d" % half)
-            products_to_sbuf(y, w2_codes, w2_sc, z_codes[:, targets], z_scales[:, targets])
-            nc.sync.dma_start(out=rows_out[:, :, targets], in_=y[:])
-            yb = tile([P, P, PACK], BF16, "y_bf%d" % half)
-            nc.vector.tensor_copy(out=woven(yb[:]), in_=by_lines(y[:]))
-            quantize_into(y_codes[:, targets], y_scales[:, targets], yb[:])
-            nc.sync.dma_start(out=words_out[:, targets], in_=y_codes[:, targets])
+        first, second = slice(0, P), slice(P, V)
+        y0 = tile([P, PACK, P], F32, "y0")
+        products_to_sbuf(y0, w2_codes, w2_sc, z_codes[:, first], z_scales[:, first])
+        nc.sync.dma_start(out=rows_out[:, :, first], in_=y0[:])
+        nc.vector.tensor_copy(out=woven(yb[:, first, :]), in_=by_lines(y0[:]))
+        banks = []
+        for pair in range(PACK // 2):
+            banks.append(bank([P, 2, P]))
+            for u in range(2):
+                product(banks[pair][:, u, :], w2_codes, w2_sc, 2 * pair + u, z_codes[:, second], z_scales[:, second])
+            nc.scalar.copy(
+                out=yb[:, second, 2 * pair : 2 * pair + 2], in_=banks[pair][:].rearrange("p u v -> p v u")
+            )
+        y1 = [tile([P, 2, P], F32, "y1_%d" % pair) for pair in range(PACK // 2)]
+        nc.vector.tensor_copy(out=y1[0][:], in_=banks[0][:])
+        nc.sync.dma_start(out=rows_out[:, 0:2, second], in_=y1[0][:])
+        nc.scalar.copy(out=y1[1][:], in_=banks[1][:])
+        nc.sync.dma_start(out=rows_out[:, 2:4, second], in_=y1[1][:])
+        for targets in (first, second):
+            quantize_into(y_codes[:, targets], y_scales[:, targets], yb[:, targets, :])
+        nc.scalar.dma_start(out=out_1[0].rearrange("p c r -> p (c r)").bitcast(I32), in_=y_codes[:])
         for q in range(BLOCKS // PACK):
             queue = nc.sync if q % 2 == 0 else nc.scalar
             queue.dma_start(

@@ -35,7 +35,8 @@ def tile_picked_dime_none_po_kernel(
     with ExitStack() as ctx:
         lists = ctx.enter_context(tc.tile_pool(name="lists", bufs=1))
         sb = ctx.enter_context(tc.tile_pool(name="sb", bufs=1))
-        psum = ctx.enter_context(tc.psum_pool(name="psum", bufs=PSUM_BANKS))
+        psum = ctx.enter_context(tc.psum_pool(name="psum", bufs=PSUM_BANKS - 1))
+        psum_last = ctx.enter_context(tc.psum_pool(name="psum_last", bufs=1))
 
         def tile(shape, dtype, name, pool=sb):
             return pool.tile(shape, dtype, name=name, align_bytes=64)
@@ -185,21 +186,46 @@ def tile_picked_dime_none_po_kernel(
         a1_codes, a1_scales = quantize(a_bf1, V, "a1")
         w2_codes = tile_over("a_bf1", [P, H], I32, "w2_codes")
         deal(w2_codes, w2w_raw, LINE_WORDS)
-        f1 = tile([P, PACK, V], F32, "f1")
-        products_to_sbuf(f1, w3_codes, w3_scales, a1_codes[:], a1_scales[:])
+        f1 = [tile([P, V], F32, "f1_%d" % t) for t in range(PACK - 1)]
+        for t in range(PACK - 1):
+            acc = bank([P, V])
+            product(acc[:], w3_codes, w3_scales, t, a1_codes[:], a1_scales[:])
+            nc.scalar.copy(out=f1[t][:], in_=acc[:])
+        f1_last = psum_last.tile([P, V], F32, name="f1_last", tag="last")
+        product(f1_last[:], w3_codes, w3_scales, PACK - 1, a1_codes[:], a1_scales[:])
+        f1_last_halves = [tile([P, P], F32, "f1_last0")]
+        nc.scalar.copy(out=f1_last_halves[0][:], in_=f1_last[:, :P])
 
-        terms = []
-        for d, f in enumerate((f0, f1)):
-            terms.append(tile([P, PACK, V], F32, "terms%d" % d))
-            for t in range(PACK):
-                last = d == 1 and t == PACK - 1
-                for v0, v1 in ((0, P), (P, V)) if last else ((0, V),):
-                    nc.vector.tensor_tensor(
-                        out=terms[d][:, t, v0:v1],
-                        in0=h[t][:].indirect(pos_t[d][:, v0 // STRIPE : v1 // STRIPE]),
-                        in1=f[:, t, v0:v1],
-                        op=MULT,
-                    )
+        terms = [tile([P, PACK, V], F32, "terms%d" % d) for d in range(2)]
+
+        def fetch(d, t, f, v0, v1):
+            nc.vector.tensor_tensor(
+                out=terms[d][:, t, v0:v1],
+                in0=h[t][:].indirect(pos_t[d][:, v0 // STRIPE : v1 // STRIPE]),
+                in1=f,
+                op=MULT,
+            )
+
+        for t in range(PACK):
+            fetch(0, t, f0[:, t, :], 0, V)
+        for t in range(2):
+            fetch(1, t, f1[t][:], 0, V)
+        f1_last_halves.append(tile_over("f1_1", [P, P], F32, "f1_last1"))
+        nc.scalar.copy(out=f1_last_halves[1][:], in_=f1_last[:, P:])
+        warm = psum_last.tile([P, S], F32, name="warm", tag="last")
+        for u in range(2):
+            nc.tensor.matmul_mx(
+                out=warm[:],
+                lhsT=w1_codes[:, u * P : (u + 1) * P].bitcast(FP8X4),
+                lhsT_scale=w1_scales[:, u * P : (u + 1) * P],
+                rhs=xw[:].bitcast(FP8X4),
+                rhs_scale=xs[:],
+                start=u == 0,
+                stop=u == 1,
+            )
+        fetch(1, 2, f1[2][:], 0, V)
+        for half in range(2):
+            fetch(1, PACK - 1, f1_last_halves[half][:], half * P, (half + 1) * P)
 
         zb = tile([P, V, PACK], BF16, "z_bf")
         z_codes = tile([P, V], U32, "z_codes")
@@ -226,29 +252,17 @@ def tile_picked_dime_none_po_kernel(
 
         y_codes = tile([P, V], I32, "y_codes")
         y_scales = tile([P, V], U8, "y_scales")
-        yb = tile([P, V, PACK], BF16, "y_bf")
         rows_out = out_0.rearrange("(p t) v -> p t v", t=PACK)
-        first, second = slice(0, P), slice(P, V)
-        y0 = tile([P, PACK, P], F32, "y0")
-        products_to_sbuf(y0, w2_codes, w2_sc, z_codes[:, first], z_scales[:, first])
-        nc.sync.dma_start(out=rows_out[:, :, first], in_=y0[:])
-        nc.vector.tensor_copy(out=woven(yb[:, first, :]), in_=by_lines(y0[:]))
-        banks = []
-        for pair in range(PACK // 2):
-            banks.append(bank([P, 2, P]))
-            for u in range(2):
-                product(banks[pair][:, u, :], w2_codes, w2_sc, 2 * pair + u, z_codes[:, second], z_scales[:, second])
-            nc.scalar.copy(
-                out=yb[:, second, 2 * pair : 2 * pair + 2], in_=banks[pair][:].rearrange("p u v -> p v u")
-            )
-        y1 = [tile([P, 2, P], F32, "y1_%d" % pair) for pair in range(PACK // 2)]
-        nc.vector.tensor_copy(out=y1[0][:], in_=banks[0][:])
-        nc.sync.dma_start(out=rows_out[:, 0:2, second], in_=y1[0][:])
-        nc.scalar.copy(out=y1[1][:], in_=banks[1][:])
-        nc.sync.dma_start(out=rows_out[:, 2:4, second], in_=y1[1][:])
-        for targets in (first, second):
-            quantize_into(y_codes[:, targets], y_scales[:, targets], yb[:, targets, :])
-        nc.scalar.dma_start(out=out_1[0].rearrange("p c r -> p (c r)").bitcast(I32), in_=y_codes[:])
+        words_out = out_1[0].rearrange("p c r -> p (c r)").bitcast(I32)
+        for half in range(2):
+            targets = slice(half * P, (half + 1) * P)
+            y = tile([P, PACK, P], F32, "y%d" % half)
+            products_to_sbuf(y, w2_codes, w2_sc, z_codes[:, targets], z_scales[:, targets])
+            nc.sync.dma_start(out=rows_out[:, :, targets], in_=y[:])
+            yb = tile([P, P, PACK], BF16, "y_bf%d" % half)
+            nc.vector.tensor_copy(out=woven(yb[:]), in_=by_lines(y[:]))
+            quantize_into(y_codes[:, targets], y_scales[:, targets], yb[:])
+            nc.sync.dma_start(out=words_out[:, targets], in_=y_codes[:, targets])
         for q in range(BLOCKS // PACK):
             queue = nc.sync if q % 2 == 0 else nc.scalar
             queue.dma_start(

@@ -35,14 +35,13 @@ def tile_picked_dime_none_po_kernel(
     with ExitStack() as ctx:
         lists = ctx.enter_context(tc.tile_pool(name="lists", bufs=1))
         sb = ctx.enter_context(tc.tile_pool(name="sb", bufs=1))
-        psum = ctx.enter_context(tc.psum_pool(name="psum", bufs=PSUM_BANKS - 1))
-        psum_last = ctx.enter_context(tc.psum_pool(name="psum_last", bufs=1))
+        psum = ctx.enter_context(tc.psum_pool(name="psum", bufs=PSUM_BANKS))
 
         def tile(shape, dtype, name, pool=sb):
             return pool.tile(shape, dtype, name=name, align_bytes=64)
 
-        def tile_over(earlier, shape, dtype, name):
-            return sb.tile(shape, dtype, name=name, tag=earlier, align_bytes=64)
+        def tile_over(earlier, shape, dtype, name, pool=sb):
+            return pool.tile(shape, dtype, name=name, tag=earlier, align_bytes=64)
 
         def bank(shape):
             return psum.tile(shape, F32, name="bank", tag="bank")
@@ -133,7 +132,7 @@ def tile_picked_dime_none_po_kernel(
             nc.vector.memset(w2s_raw[:].bitcast(I32), 0)
             xs = tile([P, S], U8, "xs")
             nc.vector.memset(xs[:].bitcast(I32), 0)
-            a_raw0 = load_rows(sb, aT, slice(0, V), "a_raw0")
+            a_raw0 = load_rows(first, aT, slice(0, V), "a_raw0")
             offs_t = load_list(offs, S, "offs_t")
             load_scale_rows(xs_all, x_scales)
             pos_t = [load_list(pos1, V, "pos1_t"), load_list(pos2, V, "pos2_t")]
@@ -148,89 +147,76 @@ def tile_picked_dime_none_po_kernel(
             w2s_dealt = tile([P, H], U8, "w2s_dealt")
             deal(w2s_dealt, w2s_raw, LINE_BYTES)
 
+            a_bf0 = tile([P, V, PACK], BF16, "a_bf0", first)
+            nc.scalar.copy(out=woven(a_bf0[:]), in_=by_lines(a_raw0[:]))
+            a0_codes, a0_scales = quantize(a_bf0, V, "a0")
+
         later = ctx.enter_context(tc.tile_pool(name="later", bufs=1))
-        a_raw1 = [load_rows(later, aT, slice(V + s * P, V + (s + 1) * P), "a_raw1_%d" % s) for s in range(2)]
-        w2w_raw = load_words(later, w2_words, H, "w2w_raw")
-        w2_sc = tile([P, H], U8, "w2_sc", later)
-        nc.vector.memset(w2_sc[:].bitcast(I32), 0)
-        place_scale_rows(nc.sync, w2_sc, w2s_dealt)
+        with tc.tile_pool(name="piece", bufs=1) as piece:
+            a_raw1 = [
+                load_rows(pool, aT, slice(V + s * P, V + (s + 1) * P), "a_raw1_%d" % s)
+                for s, pool in enumerate((piece, later))
+            ]
+            w2w_raw = load_words(later, w2_words, H, "w2w_raw")
+            w2_sc = tile([P, H], U8, "w2_sc", later)
+            nc.vector.memset(w2_sc[:].bitcast(I32), 0)
+            place_scale_rows(nc.sync, w2_sc, w2s_dealt)
 
-        a_bf0 = tile([P, V, PACK], BF16, "a_bf0")
-        nc.scalar.copy(out=woven(a_bf0[:]), in_=by_lines(a_raw0[:]))
-        a0_codes, a0_scales = quantize(a_bf0, V, "a0")
-        w3_codes, w3_scales = quantize(round_dealt(w3_raw, "w3"), H, "w3")
-        w1_codes, w1_scales = quantize(round_dealt(w1_raw, "w1"), H, "w1")
-        f0 = tile_over("w1_raw", [P, PACK, V], F32, "f0")
-        products_to_sbuf(f0, w3_codes, w3_scales, a0_codes[:], a0_scales[:])
+            w3_codes, w3_scales = quantize(round_dealt(w3_raw, "w3"), H, "w3")
+            w1_codes, w1_scales = quantize(round_dealt(w1_raw, "w1"), H, "w1")
+            f0 = tile_over("w1_raw", [P, PACK, V], F32, "f0")
+            products_to_sbuf(f0, w3_codes, w3_scales, a0_codes[:], a0_scales[:])
 
-        xw = tile([P, S], U32, "xw")
-        for c0 in range(0, S, WORD_GATHER):
-            nc.vector.tensor_copy(
-                out=xw[:, c0 : c0 + WORD_GATHER],
-                in_=xw_all[:].bitcast(U32).indirect(offs_t[:, c0 // STRIPE : (c0 + WORD_GATHER) // STRIPE]),
-            )
-        a_bf1 = tile([P, V, PACK], BF16, "a_bf1")
-        nc.scalar.copy(out=woven(a_bf1[:, :P, :]), in_=by_lines(a_raw1[0][:]))
-        nc.vector.tensor_copy(out=woven(a_bf1[:, P:, :]), in_=by_lines(a_raw1[1][:]))
+            xw = tile([P, S], U32, "xw")
+            for c0 in range(0, S, WORD_GATHER):
+                nc.vector.tensor_copy(
+                    out=xw[:, c0 : c0 + WORD_GATHER],
+                    in_=xw_all[:].bitcast(U32).indirect(offs_t[:, c0 // STRIPE : (c0 + WORD_GATHER) // STRIPE]),
+                )
 
-        h = []
+            a_bf1 = tile([P, V, PACK], BF16, "a_bf1")
+            a1_codes = tile([P, V], U32, "a1_codes")
+            a1_scales = tile([P, V], U8, "a1_scales")
+            nc.scalar.copy(out=woven(a_bf1[:, :P, :]), in_=by_lines(a_raw1[0][:]))
+            nc.vector.tensor_copy(out=woven(a_bf1[:, P:, :]), in_=by_lines(a_raw1[1][:]))
+            for cols in (slice(0, P), slice(P, V)):
+                quantize_into(a1_codes[:, cols], a1_scales[:, cols], a_bf1[:, cols, :])
+            w2_codes = tile_over("a_raw1_1", [P, H], I32, "w2_codes", later)
+            deal(w2_codes, w2w_raw, LINE_WORDS)
+
+        h_pool = ctx.enter_context(tc.tile_pool(name="h_pool", bufs=1))
+        h = [tile([P, S], F32, "h%d" % t, h_pool) for t in range(PACK)]
         for t in range(PACK):
-            h.append(tile([P, S], F32, "h%d" % t))
-            edges = (0, WORD_GATHER, WORD_GATHER + P, S) if t == 0 else (0, S)
+            edges = (0, WORD_GATHER, WORD_GATHER + P, S) if t == 0 else (0, S // 2, S)
             for c0, c1 in zip(edges[:-1], edges[1:]):
                 entries = slice(c0, c1)
                 acc = bank([P, c1 - c0])
                 product(acc[:], w1_codes, w1_scales, t, xw[:, entries], xs[:, entries])
                 nc.scalar.activation(out=h[t][:, entries], in_=acc[:], func=SILU)
 
-        a1_codes, a1_scales = quantize(a_bf1, V, "a1")
-        w2_codes = tile_over("a_bf1", [P, H], I32, "w2_codes")
-        deal(w2_codes, w2w_raw, LINE_WORDS)
-        f1 = [tile([P, V], F32, "f1_%d" % t) for t in range(PACK - 1)]
-        for t in range(PACK - 1):
+        f1 = tile([P, PACK, V], F32, "f1")
+        for t in range(PACK):
             acc = bank([P, V])
             product(acc[:], w3_codes, w3_scales, t, a1_codes[:], a1_scales[:])
-            nc.scalar.copy(out=f1[t][:], in_=acc[:])
-        f1_last = psum_last.tile([P, V], F32, name="f1_last", tag="last")
-        product(f1_last[:], w3_codes, w3_scales, PACK - 1, a1_codes[:], a1_scales[:])
-        f1_last_halves = [tile([P, P], F32, "f1_last0")]
-        nc.scalar.copy(out=f1_last_halves[0][:], in_=f1_last[:, :P])
+            nc.scalar.copy(out=f1[:, t, :], in_=acc[:])
 
-        terms = [tile([P, PACK, V], F32, "terms%d" % d) for d in range(2)]
-
-        def fetch(d, t, f, v0, v1):
-            nc.vector.tensor_tensor(
-                out=terms[d][:, t, v0:v1],
-                in0=h[t][:].indirect(pos_t[d][:, v0 // STRIPE : v1 // STRIPE]),
-                in1=f,
-                op=MULT,
-            )
-
-        for t in range(PACK):
-            fetch(0, t, f0[:, t, :], 0, V)
-        for t in range(2):
-            fetch(1, t, f1[t][:], 0, V)
-        f1_last_halves.append(tile_over("f1_1", [P, P], F32, "f1_last1"))
-        nc.scalar.copy(out=f1_last_halves[1][:], in_=f1_last[:, P:])
-        warm = psum_last.tile([P, S], F32, name="warm", tag="last")
-        for u in range(2):
-            nc.tensor.matmul_mx(
-                out=warm[:],
-                lhsT=w1_codes[:, u * P : (u + 1) * P].bitcast(FP8X4),
-                lhsT_scale=w1_scales[:, u * P : (u + 1) * P],
-                rhs=xw[:].bitcast(FP8X4),
-                rhs_scale=xs[:],
-                start=u == 0,
-                stop=u == 1,
-            )
-        fetch(1, 2, f1[2][:], 0, V)
-        for half in range(2):
-            fetch(1, PACK - 1, f1_last_halves[half][:], half * P, (half + 1) * P)
+        terms = []
+        for d, f in enumerate((f0, f1)):
+            terms.append(tile([P, PACK, V], F32, "terms%d" % d))
+            for t in range(PACK):
+                last = d == 1 and t == PACK - 1
+                for v0, v1 in ((0, P), (P, V)) if last else ((0, V),):
+                    nc.vector.tensor_tensor(
+                        out=terms[d][:, t, v0:v1],
+                        in0=h[t][:].indirect(pos_t[d][:, v0 // STRIPE : v1 // STRIPE]),
+                        in1=f[:, t, v0:v1],
+                        op=MULT,
+                    )
 
         zb = tile([P, V, PACK], BF16, "z_bf")
         z_codes = tile([P, V], U32, "z_codes")
         z_scales = tile([P, V], U8, "z_scales")
-        pieces = (slice(0, P), slice(P, P + P // 2), slice(P + P // 2, V))
+        first_half, third_quarter, last_quarter = slice(0, P), slice(P, P + P // 2), slice(P + P // 2, V)
 
         def add_terms(targets):
             nc.vector.tensor_tensor(
@@ -243,12 +229,12 @@ def tile_picked_dime_none_po_kernel(
         def quantize_z(targets):
             quantize_into(z_codes[:, targets], z_scales[:, targets], zb[:, targets, :])
 
-        add_terms(pieces[0])
-        add_terms(pieces[1])
-        quantize_z(pieces[0])
-        add_terms(pieces[2])
-        quantize_z(pieces[1])
-        quantize_z(pieces[2])
+        add_terms(first_half)
+        add_terms(third_quarter)
+        quantize_z(first_half)
+        add_terms(last_quarter)
+        quantize_z(third_quarter)
+        quantize_z(last_quarter)
 
         y_codes = tile([P, V], I32, "y_codes")
         y_scales = tile([P, V], U8, "y_scales")
@@ -264,7 +250,7 @@ def tile_picked_dime_none_po_kernel(
             quantize_into(y_codes[:, targets], y_scales[:, targets], yb[:])
             nc.sync.dma_start(out=words_out[:, targets], in_=y_codes[:, targets])
         for q in range(BLOCKS // PACK):
-            queue = nc.sync if q % 2 == 0 else nc.scalar
+            queue = nc.scalar if q == 0 else nc.sync
             queue.dma_start(
                 out=out_2[0, PACK * q : PACK * (q + 1), :].bitcast(I32),
                 in_=y_scales[QUADRANT * q : QUADRANT * q + PACK, :].bitcast(I32),

@@ -15,6 +15,7 @@ FP8X4 = mybir.dt.float8_e4m3fn_x4
 MULT = mybir.AluOpType.mult
 ADD = mybir.AluOpType.add
 SILU = mybir.ActivationFunctionType.Silu
+COPY = mybir.ActivationFunctionType.Copy
 
 P = 128
 PACK = 4
@@ -120,133 +121,160 @@ def tile_picked_dime_none_po_kernel(
                     product(acc[:, u, :], w_codes, w_scales, 2 * pair + u, codes, scales)
                 nc.scalar.copy(out=held[:, 2 * pair : 2 * pair + 2, :], in_=acc[:])
 
-        warm_in = tile([P, 1], F32, "warm_in")
-        nc.gpsimd.memset(warm_in[:], 0.0)
-        warm_out = tile([P, 1], F32, "warm_out")
-        nc.scalar.activation(out=warm_out[:], in_=warm_in[:], func=SILU)
+        def load_scale_quadrants(queue, scales, src):
+            for q in range(BLOCKS // PACK):
+                queue.dma_start(
+                    out=scales[QUADRANT * q : QUADRANT * q + PACK, :].bitcast(I32),
+                    in_=src[0, PACK * q : PACK * (q + 1), :].bitcast(I32),
+                )
 
         with tc.tile_pool(name="first", bufs=1) as first:
             xs_all = tile([P, T], U8, "xs_all", first)
-            nc.vector.memset(xs_all[:].bitcast(I32), 0)
-            w2s_raw = tile([P, H], U8, "w2s_raw")
-            nc.vector.memset(w2s_raw[:].bitcast(I32), 0)
-            xs = tile([P, S], U8, "xs")
-            nc.vector.memset(xs[:].bitcast(I32), 0)
-            a_raw0 = load_rows(first, aT, slice(0, V), "a_raw0")
+            nc.sync.dma_start(
+                out=xs_all[0:QUADRANT, :].bitcast(I32),
+                in_=x_scales[0].bitcast(I32).unsqueeze(1).broadcast_to([BLOCKS, 2, T // 4]),
+            )
+            nc.vector.memset(xs_all[QUADRANT : 2 * QUADRANT, :].bitcast(I32), 0)
+            nc.vector.memset(xs_all[2 * QUADRANT :, :].bitcast(I32), 0)
             offs_t = load_list(offs, S, "offs_t")
-            load_scale_rows(xs_all, x_scales)
-            pos_t = [load_list(pos1, V, "pos1_t"), load_list(pos2, V, "pos2_t")]
-            load_scale_rows(w2s_raw, w2_scales)
-            w3_raw = load_rows(sb, w3, slice(0, H), "w3_raw")
             w1_raw = load_rows(sb, w1, slice(0, H), "w1_raw")
             xw_all = load_words(sb, x_words, T, "xw_all")
+            pos_t = [load_list(pos1, V, "pos1_t"), load_list(pos2, V, "pos2_t")]
+            xs = tile([P, S], U8, "xs")
+            nc.vector.memset(xs[:].bitcast(I32), 0)
+
+            warm_in = tile([P, 1], F32, "warm_in")
+            nc.vector.memset(warm_in[:], 0.0)
+            warm_out = tile([P, 1], F32, "warm_out")
+            nc.scalar.activation(out=warm_out[:], in_=warm_in[:], func=SILU)
 
             xs_rows = tile([P, S], U8, "xs_rows")
             nc.vector.tensor_copy(out=xs_rows[:], in_=xs_all[:].indirect(offs_t[:]))
-            place_scale_rows(nc.scalar, xs, xs_rows)
-            w2s_dealt = tile([P, H], U8, "w2s_dealt")
-            deal(w2s_dealt, w2s_raw, LINE_BYTES)
-
-            a_bf0 = tile([P, V, PACK], BF16, "a_bf0", first)
-            nc.scalar.copy(out=woven(a_bf0[:]), in_=by_lines(a_raw0[:]))
-            a0_codes, a0_scales = quantize(a_bf0, V, "a0")
-
-        later = ctx.enter_context(tc.tile_pool(name="later", bufs=1))
-        with tc.tile_pool(name="piece", bufs=1) as piece:
-            a_raw1 = [
-                load_rows(pool, aT, slice(V + s * P, V + (s + 1) * P), "a_raw1_%d" % s)
-                for s, pool in enumerate((piece, later))
-            ]
-            w2w_raw = load_words(later, w2_words, H, "w2w_raw")
-            w2_sc = tile([P, H], U8, "w2_sc", later)
-            nc.vector.memset(w2_sc[:].bitcast(I32), 0)
-            place_scale_rows(nc.sync, w2_sc, w2s_dealt)
-
-            w3_codes, w3_scales = quantize(round_dealt(w3_raw, "w3"), H, "w3")
-            w1_codes, w1_scales = quantize(round_dealt(w1_raw, "w1"), H, "w1")
-            f0 = tile_over("w1_raw", [P, PACK, V], F32, "f0")
-            products_to_sbuf(f0, w3_codes, w3_scales, a0_codes[:], a0_scales[:])
-
-            xw = tile([P, S], U32, "xw")
-            for c0 in range(0, S, WORD_GATHER):
-                nc.vector.tensor_copy(
-                    out=xw[:, c0 : c0 + WORD_GATHER],
-                    in_=xw_all[:].bitcast(U32).indirect(offs_t[:, c0 // STRIPE : (c0 + WORD_GATHER) // STRIPE]),
+            for q in range(BLOCKS // PACK):
+                nc.sync.dma_start(
+                    out=xs[QUADRANT * q : QUADRANT * q + PACK, :].bitcast(I32),
+                    in_=xs_rows[2 * PACK * q : 2 * PACK * (q + 1) : 2, :].bitcast(I32),
                 )
 
-            a_bf1 = tile([P, V, PACK], BF16, "a_bf1")
-            a1_codes = tile([P, V], U32, "a1_codes")
-            a1_scales = tile([P, V], U8, "a1_scales")
-            nc.scalar.copy(out=woven(a_bf1[:, :P, :]), in_=by_lines(a_raw1[0][:]))
-            nc.vector.tensor_copy(out=woven(a_bf1[:, P:, :]), in_=by_lines(a_raw1[1][:]))
-            for cols in (slice(0, P), slice(P, V)):
-                quantize_into(a1_codes[:, cols], a1_scales[:, cols], a_bf1[:, cols, :])
-            w2_codes = tile_over("a_raw1_1", [P, H], I32, "w2_codes", later)
-            deal(w2_codes, w2w_raw, LINE_WORDS)
+        later = ctx.enter_context(tc.tile_pool(name="later", bufs=1))
+        w3_raw = load_rows(later, w3, slice(0, H), "w3_raw")
+        a_raw = load_rows(later, aT, slice(0, U), "a_raw")
+        w2w_raw = load_words(later, w2_words, H, "w2w_raw")
+        w2s_raw = tile([P, H], U8, "w2s_raw", later)
+        nc.vector.memset(w2s_raw[:].bitcast(I32), 0)
+        load_scale_quadrants(nc.sync, w2s_raw, w2_scales)
 
-        h_pool = ctx.enter_context(tc.tile_pool(name="h_pool", bufs=1))
-        h = [tile([P, S], F32, "h%d" % t, h_pool) for t in range(PACK)]
-        for t in range(PACK):
-            edges = (0, WORD_GATHER, WORD_GATHER + P, S) if t == 0 else (0, S // 2, S)
-            for c0, c1 in zip(edges[:-1], edges[1:]):
-                entries = slice(c0, c1)
-                acc = bank([P, c1 - c0])
-                product(acc[:], w1_codes, w1_scales, t, xw[:, entries], xs[:, entries])
-                nc.scalar.activation(out=h[t][:, entries], in_=acc[:], func=SILU)
+        def quantize_pairs(grouped, name):
+            codes = tile([P, H], U32, name + "_codes")
+            scales = tile([P, H], U8, name + "_scales")
+            for pair in range(2):
+                cols = slice(pair * 2 * P, (pair + 1) * 2 * P)
+                quantize_into(codes[:, cols], scales[:, cols], grouped[:, cols, :])
+            return codes, scales
 
-        f1 = tile([P, PACK, V], F32, "f1")
-        for t in range(PACK):
-            acc = bank([P, V])
-            product(acc[:], w3_codes, w3_scales, t, a1_codes[:], a1_scales[:])
-            nc.scalar.copy(out=f1[:, t, :], in_=acc[:])
+        w1_codes, w1_scales = quantize_pairs(round_dealt(w1_raw, "w1"), "w1")
 
-        terms = []
-        for d, f in enumerate((f0, f1)):
-            terms.append(tile([P, PACK, V], F32, "terms%d" % d))
-            for t in range(PACK):
-                last = d == 1 and t == PACK - 1
-                for v0, v1 in ((0, P), (P, V)) if last else ((0, V),):
-                    nc.vector.tensor_tensor(
-                        out=terms[d][:, t, v0:v1],
-                        in0=h[t][:].indirect(pos_t[d][:, v0 // STRIPE : v1 // STRIPE]),
-                        in1=f[:, t, v0:v1],
-                        op=MULT,
-                    )
-
-        zb = tile([P, V, PACK], BF16, "z_bf")
-        z_codes = tile([P, V], U32, "z_codes")
-        z_scales = tile([P, V], U8, "z_scales")
-        first_half, third_quarter, last_quarter = slice(0, P), slice(P, P + P // 2), slice(P + P // 2, V)
-
-        def add_terms(targets):
-            nc.vector.tensor_tensor(
-                out=woven(zb[:, targets, :]),
-                in0=by_lines(terms[0][:, :, targets]),
-                in1=by_lines(terms[1][:, :, targets]),
-                op=ADD,
+        xw = tile([P, S], U32, "xw")
+        for c0 in range(0, S, WORD_GATHER):
+            nc.vector.tensor_copy(
+                out=xw[:, c0 : c0 + WORD_GATHER],
+                in_=xw_all[:].bitcast(U32).indirect(offs_t[:, c0 // STRIPE : (c0 + WORD_GATHER) // STRIPE]),
             )
 
-        def quantize_z(targets):
-            quantize_into(z_codes[:, targets], z_scales[:, targets], zb[:, targets, :])
+        h = [tile([P, S], F32, "h%d" % t) for t in range(PACK)]
+        for t, c0, c1 in ((0, 0, 256), (1, 0, 256), (0, 256, 512), (1, 256, 512), (2, 0, 512), (3, 0, 512)):
+            entries = slice(c0, c1)
+            acc = bank([P, c1 - c0])
+            product(acc[:], w1_codes, w1_scales, t, xw[:, entries], xs[:, entries])
+            nc.scalar.activation(out=h[t][:, entries], in_=acc[:], func=SILU)
 
-        add_terms(first_half)
-        add_terms(third_quarter)
-        quantize_z(first_half)
-        add_terms(last_quarter)
-        quantize_z(third_quarter)
-        quantize_z(last_quarter)
+        picked = [tile([P, 2, 2, V], F32, "picked%d" % pair) for pair in range(2)]
+
+        def gather(t, d, v0, v1):
+            nc.scalar.activation(
+                out=picked[t // 2][:, t % 2, d, v0:v1],
+                in_=h[t][:].indirect(pos_t[d][:, v0 // STRIPE : v1 // STRIPE]),
+                func=COPY,
+            )
+
+        for slots, v0, v1 in (((0, 1), 0, V), ((2, 3), 0, P), ((2, 3), P, V)):
+            for t in slots:
+                for d in range(2):
+                    gather(t, d, v0, v1)
+
+        w3_bf = tile([P, H, PACK], BF16, "w3_bf")
+        nc.vector.tensor_copy(
+            out=w3_bf[:].rearrange("p (t m) j -> p m t j", t=PACK),
+            in_=w3_raw[:].rearrange("p j (m t) -> p m t j", t=PACK),
+        )
+        w3_codes, w3_scales = quantize_pairs(w3_bf, "w3")
+
+        a_bf = [tile([P, 2, P, PACK], BF16, "a_bf%d" % half) for half in range(2)]
+        a_codes = [tile([P, V], U32, "a_codes%d" % half) for half in range(2)]
+        a_scales = [tile([P, V], U8, "a_scales%d" % half) for half in range(2)]
+
+        def round_angles(half, d):
+            c0 = d * V + half * P
+            nc.vector.tensor_copy(out=woven(a_bf[half][:, d]), in_=by_lines(a_raw[:, :, c0 : c0 + P]))
+
+        def quantize_angles(half):
+            quantize_into(a_codes[half][:], a_scales[half][:], a_bf[half][:].rearrange("p d c j -> p (d c) j"))
+
+        round_angles(0, 0)
+        round_angles(0, 1)
+        round_angles(1, 0)
+        quantize_angles(0)
+        round_angles(1, 1)
+        w2_sc = tile([P, H], U8, "w2_sc")
+        deal(w2_sc, w2s_raw, LINE_BYTES)
+        quantize_angles(1)
 
         y_codes = tile([P, V], I32, "y_codes")
         y_scales = tile([P, V], U8, "y_scales")
         rows_out = out_0.rearrange("(p t) v -> p t v", t=PACK)
         words_out = out_1[0].rearrange("p c r -> p (c r)").bitcast(I32)
+        terms = [tile([P, PACK, 2, P], F32, "terms%d" % half) for half in range(2)]
+        zb = [tile([P, P, PACK], BF16, "z_bf%d" % half) for half in range(2)]
+
+        def multiply(half, pair):
+            acc = bank([P, 2, V])
+            for u in range(2):
+                product(acc[:, u, :], w3_codes, w3_scales, 2 * pair + u, a_codes[half][:], a_scales[half][:])
+            nc.vector.tensor_tensor(
+                out=terms[half][:, 2 * pair : 2 * pair + 2],
+                in0=picked[pair][:, :, :, half * P : (half + 1) * P],
+                in1=acc[:].rearrange("p t (d v) -> p t d v", d=2),
+                op=MULT,
+            )
+
+        def add_terms(half):
+            nc.vector.tensor_tensor(
+                out=woven(zb[half][:]),
+                in0=by_lines(terms[half][:, :, 0, :]),
+                in1=by_lines(terms[half][:, :, 1, :]),
+                op=ADD,
+            )
+
+        multiply(0, 0)
+        w2_codes = tile([P, H], I32, "w2_codes")
+        deal(w2_codes, w2w_raw, LINE_WORDS)
+        multiply(0, 1)
+        add_terms(0)
+        multiply(1, 0)
+        z = [quantize(zb[0], P, "z0")]
+        multiply(1, 1)
+        add_terms(1)
+        z.append(quantize(zb[1], P, "z1"))
         for half in range(2):
             targets = slice(half * P, (half + 1) * P)
             y = tile([P, PACK, P], F32, "y%d" % half)
-            products_to_sbuf(y, w2_codes, w2_sc, z_codes[:, targets], z_scales[:, targets])
+            products_to_sbuf(y, w2_codes, w2_sc, z[half][0][:], z[half][1][:])
             nc.sync.dma_start(out=rows_out[:, :, targets], in_=y[:])
             yb = tile([P, P, PACK], BF16, "y_bf%d" % half)
-            nc.vector.tensor_copy(out=woven(yb[:]), in_=by_lines(y[:]))
+            if half == 0:
+                nc.scalar.copy(out=woven(yb[:]), in_=by_lines(y[:]))
+            else:
+                nc.vector.tensor_copy(out=woven(yb[:]), in_=by_lines(y[:]))
             quantize_into(y_codes[:, targets], y_scales[:, targets], yb[:])
             nc.sync.dma_start(out=words_out[:, targets], in_=y_codes[:, targets])
         for q in range(BLOCKS // PACK):

@@ -63,16 +63,6 @@ def tile_picked_dime_none_po_kernel(
             nc.sync.dma_start(out=words[:], in_=src[0].rearrange("p c r -> p (c r)").bitcast(I32))
             return words
 
-        def load_scale_rows(rows, src):
-            nc.sync.dma_start(out=rows[0:BLOCKS, :].bitcast(I32), in_=src[0].bitcast(I32))
-
-        def place_scale_rows(queue, scales, rows):
-            for q in range(BLOCKS // PACK):
-                queue.dma_start(
-                    out=scales[QUADRANT * q : QUADRANT * q + PACK, :].bitcast(I32),
-                    in_=rows[PACK * q : PACK * (q + 1), :].bitcast(I32),
-                )
-
         def round_dealt(raw, name):
             grouped = tile([P, H, PACK], BF16, name + "_bf")
             dealt = grouped[:].rearrange("p (t m) j -> p m t j", t=PACK)
@@ -121,27 +111,39 @@ def tile_picked_dime_none_po_kernel(
                     product(acc[:, u, :], w_codes, w_scales, 2 * pair + u, codes, scales)
                 nc.scalar.copy(out=held[:, 2 * pair : 2 * pair + 2, :], in_=acc[:])
 
-        def load_scale_quadrants(queue, scales, src):
+        def load_scale_rows(src, columns, name, pool):
+            rows = tile([P, columns], U8, name, pool)
+            nc.sync.dma_start(out=rows[BLOCKS : 2 * BLOCKS, :].bitcast(I32), in_=src[0].bitcast(I32))
+            for p0, p1 in ((0, BLOCKS), (QUADRANT, 2 * QUADRANT), (2 * QUADRANT, P)):
+                nc.vector.memset(rows[p0:p1, :].bitcast(I32), 0)
+            return rows
+
+        def place_scale_rows(scales, rows):
             for q in range(BLOCKS // PACK):
-                queue.dma_start(
+                nc.sync.dma_start(
                     out=scales[QUADRANT * q : QUADRANT * q + PACK, :].bitcast(I32),
-                    in_=src[0, PACK * q : PACK * (q + 1), :].bitcast(I32),
+                    in_=rows[BLOCKS + PACK * q : BLOCKS + PACK * (q + 1), :].bitcast(I32),
                 )
 
+        def load_row_pairs(pool, src, name):
+            rows = src.rearrange("(p j) c -> p j c", j=PACK)
+            raws = []
+            for g in range(2):
+                raws.append(tile([P, 2, src.shape[1]], F32, "%s%d" % (name, g), pool))
+                nc.sync.dma_start(out=raws[g][:], in_=rows[:, 2 * g : 2 * g + 2, :])
+            return raws
+
         with tc.tile_pool(name="first", bufs=1) as first:
-            xs_all = tile([P, T], U8, "xs_all", first)
-            nc.sync.dma_start(
-                out=xs_all[0:QUADRANT, :].bitcast(I32),
-                in_=x_scales[0].bitcast(I32).unsqueeze(1).broadcast_to([BLOCKS, 2, T // 4]),
-            )
-            nc.vector.memset(xs_all[QUADRANT : 2 * QUADRANT, :].bitcast(I32), 0)
-            nc.vector.memset(xs_all[2 * QUADRANT :, :].bitcast(I32), 0)
+            xs_all = load_scale_rows(x_scales, T, "xs_all", first)
             offs_t = load_list(offs, S, "offs_t")
             w1_raw = load_rows(sb, w1, slice(0, H), "w1_raw")
-            xw_all = load_words(sb, x_words, T, "xw_all")
+            w2s_raw = load_scale_rows(w2_scales, H, "w2s_raw", sb)
             pos_t = [load_list(pos1, V, "pos1_t"), load_list(pos2, V, "pos2_t")]
+            xw_all = load_words(sb, x_words, T, "xw_all")
             xs = tile([P, S], U8, "xs")
             nc.vector.memset(xs[:].bitcast(I32), 0)
+            w2_sc = tile([P, H], U8, "w2_sc")
+            nc.vector.memset(w2_sc[:].bitcast(I32), 0)
 
             warm_in = tile([P, 1], F32, "warm_in")
             nc.vector.memset(warm_in[:], 0.0)
@@ -150,19 +152,15 @@ def tile_picked_dime_none_po_kernel(
 
             xs_rows = tile([P, S], U8, "xs_rows")
             nc.vector.tensor_copy(out=xs_rows[:], in_=xs_all[:].indirect(offs_t[:]))
-            for q in range(BLOCKS // PACK):
-                nc.sync.dma_start(
-                    out=xs[QUADRANT * q : QUADRANT * q + PACK, :].bitcast(I32),
-                    in_=xs_rows[2 * PACK * q : 2 * PACK * (q + 1) : 2, :].bitcast(I32),
-                )
+            place_scale_rows(xs, xs_rows)
 
         later = ctx.enter_context(tc.tile_pool(name="later", bufs=1))
-        w3_raw = load_rows(later, w3, slice(0, H), "w3_raw")
-        a_raw = load_rows(later, aT, slice(0, U), "a_raw")
+        w3_raw = load_row_pairs(later, w3, "w3_raw")
+        a_raw = load_row_pairs(later, aT, "a_raw")
         w2w_raw = load_words(later, w2_words, H, "w2w_raw")
-        w2s_raw = tile([P, H], U8, "w2s_raw", later)
-        nc.vector.memset(w2s_raw[:].bitcast(I32), 0)
-        load_scale_quadrants(nc.sync, w2s_raw, w2_scales)
+        w2s_dealt = tile([P, H], U8, "w2s_dealt")
+        deal(w2s_dealt, w2s_raw, LINE_BYTES)
+        place_scale_rows(w2_sc, w2s_dealt)
 
         def quantize_pairs(grouped, name):
             codes = tile([P, H], U32, name + "_codes")
@@ -175,14 +173,16 @@ def tile_picked_dime_none_po_kernel(
         w1_codes, w1_scales = quantize_pairs(round_dealt(w1_raw, "w1"), "w1")
 
         xw = tile([P, S], U32, "xw")
-        for c0 in range(0, S, WORD_GATHER):
+        for c0, c1 in ((0, P), (P, 2 * P), (2 * P, S)):
             nc.vector.tensor_copy(
-                out=xw[:, c0 : c0 + WORD_GATHER],
-                in_=xw_all[:].bitcast(U32).indirect(offs_t[:, c0 // STRIPE : (c0 + WORD_GATHER) // STRIPE]),
+                out=xw[:, c0:c1], in_=xw_all[:].bitcast(U32).indirect(offs_t[:, c0 // STRIPE : c1 // STRIPE])
             )
 
         h = [tile([P, S], F32, "h%d" % t) for t in range(PACK)]
-        for t, c0, c1 in ((0, 0, 256), (1, 0, 256), (0, 256, 512), (1, 256, 512), (2, 0, 512), (3, 0, 512)):
+        for t, c0, c1 in (
+            [(0, 0, P), (1, 0, P), (0, P, 2 * P), (1, P, 2 * P), (2, 0, 2 * P), (3, 0, 2 * P)]
+            + [(t, 2 * P, S) for t in range(PACK)]
+        ):
             entries = slice(c0, c1)
             acc = bank([P, c1 - c0])
             product(acc[:], w1_codes, w1_scales, t, xw[:, entries], xs[:, entries])
@@ -190,93 +190,128 @@ def tile_picked_dime_none_po_kernel(
 
         picked = [tile([P, 2, 2, V], F32, "picked%d" % pair) for pair in range(2)]
 
-        def gather(t, d, v0, v1):
-            nc.scalar.activation(
-                out=picked[t // 2][:, t % 2, d, v0:v1],
-                in_=h[t][:].indirect(pos_t[d][:, v0 // STRIPE : v1 // STRIPE]),
-                func=COPY,
-            )
+        first_half, third_quarter, last_quarter = slice(0, P), slice(P, P + P // 2), slice(P + P // 2, V)
+        second_half = slice(P, V)
 
-        for slots, v0, v1 in (((0, 1), 0, V), ((2, 3), 0, P), ((2, 3), P, V)):
-            for t in slots:
-                for d in range(2):
-                    gather(t, d, v0, v1)
+        def gather(t, targets, on_vector=False):
+            for d in range(2):
+                out = picked[t // 2][:, t % 2, d, targets]
+                window = h[t][:].indirect(pos_t[d][:, targets.start // STRIPE : targets.stop // STRIPE])
+                if on_vector:
+                    nc.vector.tensor_copy(out=out, in_=window)
+                else:
+                    nc.scalar.activation(out=out, in_=window, func=COPY)
+
+        gather(0, slice(0, V))
+        gather(1, slice(0, V))
+        for targets in (first_half, third_quarter, last_quarter):
+            gather(2, targets)
+            gather(3, targets)
 
         w3_bf = tile([P, H, PACK], BF16, "w3_bf")
-        nc.vector.tensor_copy(
-            out=w3_bf[:].rearrange("p (t m) j -> p m t j", t=PACK),
-            in_=w3_raw[:].rearrange("p j (m t) -> p m t j", t=PACK),
-        )
+        for g in range(2):
+            nc.vector.tensor_copy(
+                out=w3_bf[:, :, 2 * g : 2 * g + 2].rearrange("p (t r i) j -> p r t i j", t=PACK, i=2),
+                in_=w3_raw[g][:].rearrange("p j (r i t) -> p r t i j", t=PACK, i=2),
+            )
         w3_codes, w3_scales = quantize_pairs(w3_bf, "w3")
 
-        a_bf = [tile([P, 2, P, PACK], BF16, "a_bf%d" % half) for half in range(2)]
+        a_bf = tile([P, 2, 2, P, PACK], BF16, "a_bf")
         a_codes = [tile([P, V], U32, "a_codes%d" % half) for half in range(2)]
         a_scales = [tile([P, V], U8, "a_scales%d" % half) for half in range(2)]
 
-        def round_angles(half, d):
-            c0 = d * V + half * P
-            nc.vector.tensor_copy(out=woven(a_bf[half][:, d]), in_=by_lines(a_raw[:, :, c0 : c0 + P]))
+        def round_angles(g, half):
+            nc.vector.tensor_copy(
+                out=a_bf[:, half, :, :, 2 * g : 2 * g + 2],
+                in_=a_raw[g][:].rearrange("p j (d u c) -> p u d c j", d=2, u=2)[:, half],
+            )
 
         def quantize_angles(half):
-            quantize_into(a_codes[half][:], a_scales[half][:], a_bf[half][:].rearrange("p d c j -> p (d c) j"))
+            quantize_into(a_codes[half][:], a_scales[half][:], a_bf[:, half].rearrange("p d c j -> p (d c) j"))
 
-        round_angles(0, 0)
-        round_angles(0, 1)
-        round_angles(1, 0)
-        quantize_angles(0)
-        round_angles(1, 1)
-        w2_sc = tile([P, H], U8, "w2_sc")
-        deal(w2_sc, w2s_raw, LINE_BYTES)
-        quantize_angles(1)
+        for g in range(2):
+            for half in range(2):
+                round_angles(g, half)
+        for half in range(2):
+            quantize_angles(half)
 
         y_codes = tile([P, V], I32, "y_codes")
         y_scales = tile([P, V], U8, "y_scales")
         rows_out = out_0.rearrange("(p t) v -> p t v", t=PACK)
         words_out = out_1[0].rearrange("p c r -> p (c r)").bitcast(I32)
-        terms = [tile([P, PACK, 2, P], F32, "terms%d" % half) for half in range(2)]
-        zb = [tile([P, P, PACK], BF16, "z_bf%d" % half) for half in range(2)]
+        terms = tile([P, PACK, 2, V], F32, "terms")
+        zb = tile([P, V, PACK], BF16, "z_bf")
+        z_codes = tile([P, V], U32, "z_codes")
+        z_scales = tile([P, V], U8, "z_scales")
 
-        def multiply(half, pair):
+        def filters(half, pair):
             acc = bank([P, 2, V])
             for u in range(2):
                 product(acc[:, u, :], w3_codes, w3_scales, 2 * pair + u, a_codes[half][:], a_scales[half][:])
+            return acc[:].rearrange("p t (d v) -> p t d v", d=2)
+
+        def multiply(f, pair, targets):
+            v0 = targets.start % P
             nc.vector.tensor_tensor(
-                out=terms[half][:, 2 * pair : 2 * pair + 2],
-                in0=picked[pair][:, :, :, half * P : (half + 1) * P],
-                in1=acc[:].rearrange("p t (d v) -> p t d v", d=2),
+                out=terms[:, 2 * pair : 2 * pair + 2, :, targets],
+                in0=picked[pair][:, :, :, targets],
+                in1=f[:, :, :, v0 : v0 + targets.stop - targets.start],
                 op=MULT,
             )
 
-        def add_terms(half):
+        def add_terms(targets):
             nc.vector.tensor_tensor(
-                out=woven(zb[half][:]),
-                in0=by_lines(terms[half][:, :, 0, :]),
-                in1=by_lines(terms[half][:, :, 1, :]),
+                out=woven(zb[:, targets, :]),
+                in0=by_lines(terms[:, :, 0, targets]),
+                in1=by_lines(terms[:, :, 1, targets]),
                 op=ADD,
             )
 
-        multiply(0, 0)
+        def quantize_z(targets):
+            quantize_into(z_codes[:, targets], z_scales[:, targets], zb[:, targets, :])
+
+        f = [[filters(half, pair) for pair in range(2)] for half in range(2)]
         w2_codes = tile([P, H], I32, "w2_codes")
         deal(w2_codes, w2w_raw, LINE_WORDS)
-        multiply(0, 1)
-        add_terms(0)
-        multiply(1, 0)
-        z = [quantize(zb[0], P, "z0")]
-        multiply(1, 1)
-        add_terms(1)
-        z.append(quantize(zb[1], P, "z1"))
-        for half in range(2):
-            targets = slice(half * P, (half + 1) * P)
-            y = tile([P, PACK, P], F32, "y%d" % half)
-            products_to_sbuf(y, w2_codes, w2_sc, z[half][0][:], z[half][1][:])
-            nc.sync.dma_start(out=rows_out[:, :, targets], in_=y[:])
-            yb = tile([P, P, PACK], BF16, "y_bf%d" % half)
-            if half == 0:
-                nc.scalar.copy(out=woven(yb[:]), in_=by_lines(y[:]))
-            else:
-                nc.vector.tensor_copy(out=woven(yb[:]), in_=by_lines(y[:]))
-            quantize_into(y_codes[:, targets], y_scales[:, targets], yb[:])
-            nc.sync.dma_start(out=words_out[:, targets], in_=y_codes[:, targets])
+        multiply(f[0][0], 0, first_half)
+        multiply(f[1][0], 0, second_half)
+        multiply(f[0][1], 1, first_half)
+        add_terms(first_half)
+        multiply(f[1][1], 1, third_quarter)
+        quantize_z(first_half)
+        add_terms(third_quarter)
+        multiply(f[1][1], 1, last_quarter)
+        quantize_z(third_quarter)
+        add_terms(last_quarter)
+        quantize_z(last_quarter)
+
+        y = [tile([P, PACK, P], F32, "y%d" % half) for half in range(2)]
+        yb = tile([P, V, PACK], BF16, "y_bf")
+        products_to_sbuf(y[0], w2_codes, w2_sc, z_codes[:, first_half], z_scales[:, first_half])
+        nc.sync.dma_start(out=rows_out[:, :, first_half], in_=y[0][:])
+        nc.scalar.copy(out=woven(yb[:, first_half, :]), in_=by_lines(y[0][:]))
+        for targets in (third_quarter, last_quarter):
+            acc = bank([P, PACK, P // 2])
+            for t in range(PACK):
+                product(acc[:, t, :], w2_codes, w2_sc, t, z_codes[:, targets], z_scales[:, targets])
+            nc.scalar.copy(out=y[1][:, :, targets.start - P : targets.stop - P], in_=acc[:])
+        nc.sync.dma_start(out=rows_out[:, :, second_half], in_=y[1][:])
+
+        def round_y(targets):
+            nc.vector.tensor_copy(
+                out=woven(yb[:, targets, :]), in_=by_lines(y[1][:, :, targets.start - P : targets.stop - P])
+            )
+
+        def quantize_y(targets):
+            quantize_into(y_codes[:, targets], y_scales[:, targets], yb[:, targets, :])
+
+        round_y(third_quarter)
+        quantize_y(first_half)
+        nc.sync.dma_start(out=words_out[:, first_half], in_=y_codes[:, first_half])
+        quantize_y(third_quarter)
+        round_y(last_quarter)
+        quantize_y(last_quarter)
+        nc.sync.dma_start(out=words_out[:, second_half], in_=y_codes[:, second_half])
         for q in range(BLOCKS // PACK):
             queue = nc.scalar if q == 0 else nc.sync
             queue.dma_start(

@@ -202,11 +202,14 @@ def tile_picked_dime_none_po_kernel(
                 else:
                     nc.scalar.activation(out=out, in_=window, func=COPY)
 
-        gather(0, slice(0, V))
-        gather(1, slice(0, V))
-        for targets in (first_half, third_quarter, last_quarter):
-            gather(2, targets)
-            gather(3, targets)
+        for slots, targets in (
+            (range(PACK), first_half),
+            ((0, 1), second_half),
+            ((2, 3), third_quarter),
+            ((2, 3), last_quarter),
+        ):
+            for t in slots:
+                gather(t, targets)
 
         w3_bf = tile([P, H, PACK], BF16, "w3_bf")
         for g in range(2):
@@ -244,17 +247,18 @@ def tile_picked_dime_none_po_kernel(
         z_codes = tile([P, V], U32, "z_codes")
         z_scales = tile([P, V], U8, "z_scales")
 
-        def filters(half, pair):
-            acc = bank([P, 2, V])
-            for u in range(2):
-                product(acc[:, u, :], w3_codes, w3_scales, 2 * pair + u, a_codes[half][:], a_scales[half][:])
+        def filters(half, slots):
+            acc = bank([P, len(slots), V])
+            for u, t in enumerate(slots):
+                product(acc[:, u, :], w3_codes, w3_scales, t, a_codes[half][:], a_scales[half][:])
             return acc[:].rearrange("p t (d v) -> p t d v", d=2)
 
-        def multiply(f, pair, targets):
+        def multiply(f, slots, targets):
             v0 = targets.start % P
+            u0 = slots[0] % 2
             nc.vector.tensor_tensor(
-                out=terms[:, 2 * pair : 2 * pair + 2, :, targets],
-                in0=picked[pair][:, :, :, targets],
+                out=terms[:, slots[0] : slots[-1] + 1, :, targets],
+                in0=picked[slots[0] // 2][:, u0 : u0 + len(slots), :, targets],
                 in1=f[:, :, :, v0 : v0 + targets.stop - targets.start],
                 op=MULT,
             )
@@ -270,17 +274,18 @@ def tile_picked_dime_none_po_kernel(
         def quantize_z(targets):
             quantize_into(z_codes[:, targets], z_scales[:, targets], zb[:, targets, :])
 
-        f = [[filters(half, pair) for pair in range(2)] for half in range(2)]
         w2_codes = tile([P, H], I32, "w2_codes")
         deal(w2_codes, w2w_raw, LINE_WORDS)
-        multiply(f[0][0], 0, first_half)
-        multiply(f[1][0], 0, second_half)
-        multiply(f[0][1], 1, first_half)
+        for slots in ((0,), (1,), (2, 3)):
+            multiply(filters(0, slots), slots, first_half)
+        later_filters = [filters(1, slots) for slots in ((0, 1), (2, 3))]
+        multiply(later_filters[0], (0, 1), third_quarter)
         add_terms(first_half)
-        multiply(f[1][1], 1, third_quarter)
+        multiply(later_filters[1], (2, 3), third_quarter)
         quantize_z(first_half)
+        multiply(later_filters[0], (0, 1), last_quarter)
         add_terms(third_quarter)
-        multiply(f[1][1], 1, last_quarter)
+        multiply(later_filters[1], (2, 3), last_quarter)
         quantize_z(third_quarter)
         add_terms(last_quarter)
         quantize_z(last_quarter)

@@ -111,9 +111,9 @@ def tile_picked_dime_none_po_kernel(
                     product(acc[:, u, :], w_codes, w_scales, 2 * pair + u, codes, scales)
                 nc.scalar.copy(out=held[:, 2 * pair : 2 * pair + 2, :], in_=acc[:])
 
-        def load_scale_rows(src, columns, name, pool):
+        def load_scale_rows(src, columns, name, pool, queue):
             rows = tile([P, columns], U8, name, pool)
-            nc.sync.dma_start(out=rows[BLOCKS : 2 * BLOCKS, :].bitcast(I32), in_=src[0].bitcast(I32))
+            queue.dma_start(out=rows[BLOCKS : 2 * BLOCKS, :].bitcast(I32), in_=src[0].bitcast(I32))
             for p0, p1 in ((0, BLOCKS), (QUADRANT, 2 * QUADRANT), (2 * QUADRANT, P)):
                 nc.vector.memset(rows[p0:p1, :].bitcast(I32), 0)
             return rows
@@ -134,12 +134,13 @@ def tile_picked_dime_none_po_kernel(
             return raws
 
         with tc.tile_pool(name="first", bufs=1) as first:
-            xs_all = load_scale_rows(x_scales, T, "xs_all", first)
+            xs_all = load_scale_rows(x_scales, T, "xs_all", first, nc.scalar)
             offs_t = load_list(offs, S, "offs_t")
             w1_raw = load_rows(sb, w1, slice(0, H), "w1_raw")
-            w2s_raw = load_scale_rows(w2_scales, H, "w2s_raw", sb)
-            pos_t = [load_list(pos1, V, "pos1_t"), load_list(pos2, V, "pos2_t")]
+            w2s_raw = load_scale_rows(w2_scales, H, "w2s_raw", sb, nc.scalar)
+            pos_t = [load_list(pos1, V, "pos1_t")]
             xw_all = load_words(sb, x_words, T, "xw_all")
+            pos_t.append(load_list(pos2, V, "pos2_t"))
             xs = tile([P, S], U8, "xs")
             nc.vector.memset(xs[:].bitcast(I32), 0)
             w2_sc = tile([P, H], U8, "w2_sc")

@@ -295,12 +295,12 @@ def tile_picked_dime_none_po_kernel(
         yb = tile([P, V, PACK], BF16, "y_bf")
         products_to_sbuf(y[0], w2_codes, w2_sc, z_codes[:, first_half], z_scales[:, first_half])
         nc.sync.dma_start(out=rows_out[:, :, first_half], in_=y[0][:])
-        nc.scalar.copy(out=woven(yb[:, first_half, :]), in_=by_lines(y[0][:]))
-        for targets in (third_quarter, last_quarter):
-            acc = bank([P, PACK, P // 2])
-            for t in range(PACK):
-                product(acc[:, t, :], w2_codes, w2_sc, t, z_codes[:, targets], z_scales[:, targets])
-            nc.scalar.copy(out=y[1][:, :, targets.start - P : targets.stop - P], in_=acc[:])
+        nc.vector.tensor_copy(out=woven(yb[:, first_half, :]), in_=by_lines(y[0][:]))
+        acc = bank([P, PACK, P // 2])
+        for t in range(PACK):
+            product(acc[:, t, :], w2_codes, w2_sc, t, z_codes[:, third_quarter], z_scales[:, third_quarter])
+        nc.scalar.copy(out=y[1][:, :, : P // 2], in_=acc[:])
+        products_to_sbuf(y[1][:, :, P // 2 :], w2_codes, w2_sc, z_codes[:, last_quarter], z_scales[:, last_quarter])
         nc.sync.dma_start(out=rows_out[:, :, second_half], in_=y[1][:])
 
         def round_y(targets):

@@ -36,7 +36,8 @@ def tile_picked_dime_none_po_kernel(
     with ExitStack() as ctx:
         lists = ctx.enter_context(tc.tile_pool(name="lists", bufs=1))
         sb = ctx.enter_context(tc.tile_pool(name="sb", bufs=1))
-        psum = ctx.enter_context(tc.psum_pool(name="psum", bufs=PSUM_BANKS))
+        psum = ctx.enter_context(tc.psum_pool(name="psum", bufs=PSUM_BANKS - 3))
+        psum_f = ctx.enter_context(tc.psum_pool(name="psum_f", bufs=1))
 
         def tile(shape, dtype, name, pool=sb):
             return pool.tile(shape, dtype, name=name, align_bytes=64)
@@ -220,18 +221,19 @@ def tile_picked_dime_none_po_kernel(
             )
         w3_codes, w3_scales = quantize_pairs(w3_bf, "w3")
 
-        a_bf = tile([P, 2, 2, P, PACK], BF16, "a_bf")
+        a_bf = tile([P, 2, V, PACK], BF16, "a_bf")
         a_codes = [tile([P, V], U32, "a_codes%d" % half) for half in range(2)]
         a_scales = [tile([P, V], U8, "a_scales%d" % half) for half in range(2)]
 
         def round_angles(g, half):
+            pieces = 1 + half
             nc.vector.tensor_copy(
-                out=a_bf[:, half, :, :, 2 * g : 2 * g + 2],
-                in_=a_raw[g][:].rearrange("p j (d u c) -> p u d c j", d=2, u=2)[:, half],
+                out=a_bf[:, half, :, 2 * g : 2 * g + 2].rearrange("p (q d c) j -> p q d c j", q=pieces, d=2),
+                in_=a_raw[g][:].rearrange("p j (d u q c) -> p u q d c j", d=2, u=2, q=pieces)[:, half],
             )
 
         def quantize_angles(half):
-            quantize_into(a_codes[half][:], a_scales[half][:], a_bf[:, half].rearrange("p d c j -> p (d c) j"))
+            quantize_into(a_codes[half][:], a_scales[half][:], a_bf[:, half])
 
         for g in range(2):
             for half in range(2):
@@ -248,19 +250,21 @@ def tile_picked_dime_none_po_kernel(
         z_codes = tile([P, V], U32, "z_codes")
         z_scales = tile([P, V], U8, "z_scales")
 
-        def filters(half, slots):
-            acc = bank([P, len(slots), V])
+        def multiply(slots, targets, tag, warm_up=False):
+            half, n = targets.start // P, targets.stop - targets.start
+            cols = slice(2 * (targets.start - half * P), 2 * (targets.stop - half * P))
+            whole = psum_f.tile([P, 2 * V], F32, name="filters", tag=tag)
+            acc = whole[:, : len(slots) * 2 * n].rearrange("p (t c) -> p t c", t=len(slots))
             for u, t in enumerate(slots):
-                product(acc[:, u, :], w3_codes, w3_scales, t, a_codes[half][:], a_scales[half][:])
-            return acc[:].rearrange("p t (d v) -> p t d v", d=2)
-
-        def multiply(f, slots, targets):
-            v0 = targets.start % P
+                product(acc[:, u, :], w3_codes, w3_scales, t, a_codes[half][:, cols], a_scales[half][:, cols])
+            if warm_up:
+                for t in slots:
+                    product(whole[:, V:], w3_codes, w3_scales, t, a_codes[0][:], a_scales[0][:])
             u0 = slots[0] % 2
             nc.vector.tensor_tensor(
                 out=terms[:, slots[0] : slots[-1] + 1, :, targets],
                 in0=picked[slots[0] // 2][:, u0 : u0 + len(slots), :, targets],
-                in1=f[:, :, :, v0 : v0 + targets.stop - targets.start],
+                in1=acc.rearrange("p t (d v) -> p t d v", d=2),
                 op=MULT,
             )
 
@@ -277,22 +281,22 @@ def tile_picked_dime_none_po_kernel(
 
         w2_codes = tile([P, H], I32, "w2_codes")
         deal(w2_codes, w2w_raw, LINE_WORDS)
-        for slots in ((0,), (1,), (2, 3)):
-            multiply(filters(0, slots), slots, first_half)
-        later_filters = [filters(1, slots) for slots in ((0, 1), (2, 3))]
-        multiply(later_filters[0], (0, 1), third_quarter)
+        multiply((0,), first_half, "low")
+        multiply((1,), first_half, "second")
+        multiply((2, 3), first_half, "high")
+        multiply((0, 1), third_quarter, "low")
         add_terms(first_half)
-        multiply(later_filters[1], (2, 3), third_quarter)
+        multiply((2, 3), third_quarter, "high")
         quantize_z(first_half)
-        multiply(later_filters[0], (0, 1), last_quarter)
+        multiply((0, 1), last_quarter, "low", warm_up=True)
         add_terms(third_quarter)
-        multiply(later_filters[1], (2, 3), last_quarter)
+        multiply((2, 3), last_quarter, "high")
         quantize_z(third_quarter)
         add_terms(last_quarter)
         quantize_z(last_quarter)
 
         y = [tile([P, PACK, P], F32, "y%d" % half) for half in range(2)]
-        yb = tile([P, V, PACK], BF16, "y_bf")
+        yb = tile_over("terms", [P, V, PACK], BF16, "y_bf")
         products_to_sbuf(y[0], w2_codes, w2_sc, z_codes[:, first_half], z_scales[:, first_half])
         nc.sync.dma_start(out=rows_out[:, :, first_half], in_=y[0][:])
         nc.vector.tensor_copy(out=woven(yb[:, first_half, :]), in_=by_lines(y[0][:]))

@@ -19,14 +19,22 @@ COPY = mybir.ActivationFunctionType.Copy
 
 P = 128
 PACK = 4
+NEIGHBOURS = 2
 BLOCKS = 16
 QUADRANT = 32
 STRIPE = 16
-PSUM_BANKS = 8
-WORD_GATHER = S // 2
 LINE_WORDS = 4
 LINE_BYTES = 16
 VECTOR_GROUPS = 84
+
+LOW_SLOTS, HIGH_SLOTS = (0, 1), (2, 3)
+FIRST_HALF, SECOND_HALF = slice(0, P), slice(P, V)
+THIRD_QUARTER, LAST_QUARTER = slice(P, P + P // 2), slice(P + P // 2, V)
+
+PSUM_BANKS = 8
+FILTER_BANK = 2
+LOW_BANK, HIGH_BANK = FILTER_BANK, FILTER_BANK + PACK - 1
+FIRST_HALF_BANK, THIRD_QUARTER_BANK, LAST_QUARTER_BANK = 6, 0, 3
 
 
 def tile_picked_dime_none_po_kernel(
@@ -36,23 +44,13 @@ def tile_picked_dime_none_po_kernel(
     with ExitStack() as ctx:
         lists = ctx.enter_context(tc.tile_pool(name="lists", bufs=1))
         sb = ctx.enter_context(tc.tile_pool(name="sb", bufs=1))
-        psum = ctx.enter_context(tc.psum_pool(name="psum", bufs=PSUM_BANKS - 3))
-        psum_f = ctx.enter_context(tc.psum_pool(name="psum_f", bufs=1))
+        psum = ctx.enter_context(tc.psum_pool(name="psum", bufs=1))
 
         def tile(shape, dtype, name, pool=sb):
             return pool.tile(shape, dtype, name=name, align_bytes=64)
 
-        def tile_over(earlier, shape, dtype, name, pool=sb):
-            return pool.tile(shape, dtype, name=name, tag=earlier, align_bytes=64)
-
-        def bank(shape):
-            return psum.tile(shape, F32, name="bank", tag="bank")
-
-        def load_rows(pool, src, cols, name):
-            part = src.rearrange("(p j) c -> p j c", j=PACK)[:, :, cols]
-            raw = tile(list(part.shape), F32, name, pool)
-            nc.sync.dma_start(out=raw[:], in_=part)
-            return raw
+        def bank(shape, number):
+            return psum.tile(shape, F32, name="bank", tag="bank%d" % number)
 
         def load_list(src, entries, name):
             held = lists.tile([P, entries // STRIPE], U16, name=name)
@@ -64,13 +62,27 @@ def tile_picked_dime_none_po_kernel(
             nc.sync.dma_start(out=words[:], in_=src[0].rearrange("p c r -> p (c r)").bitcast(I32))
             return words
 
-        def round_dealt(raw, name):
-            grouped = tile([P, H, PACK], BF16, name + "_bf")
-            dealt = grouped[:].rearrange("p (t m) j -> p m t j", t=PACK)
-            source = raw[:].rearrange("p j (m t) -> p m t j", t=PACK)
-            nc.vector.tensor_copy(out=dealt[:, :VECTOR_GROUPS], in_=source[:, :VECTOR_GROUPS])
-            nc.scalar.copy(out=dealt[:, VECTOR_GROUPS:], in_=source[:, VECTOR_GROUPS:])
-            return grouped
+        def load_row_pairs(pool, src, name):
+            rows = src.rearrange("(p j) c -> p j c", j=PACK)
+            raws = []
+            for g in range(2):
+                raws.append(tile([P, 2, src.shape[1]], F32, "%s%d" % (name, g), pool))
+                nc.sync.dma_start(out=raws[g][:], in_=rows[:, 2 * g : 2 * g + 2, :])
+            return raws
+
+        def load_scale_rows(src, columns, name, pool):
+            rows = tile([P, columns], U8, name, pool)
+            nc.scalar.dma_start(out=rows[BLOCKS : 2 * BLOCKS, :].bitcast(I32), in_=src[0].bitcast(I32))
+            for p0, p1 in ((0, BLOCKS), (QUADRANT, 2 * QUADRANT), (2 * QUADRANT, P)):
+                nc.vector.memset(rows[p0:p1, :].bitcast(I32), 0)
+            return rows
+
+        def place_scale_rows(scales, rows):
+            for q in range(BLOCKS // PACK):
+                nc.sync.dma_start(
+                    out=scales[QUADRANT * q : QUADRANT * q + PACK, :].bitcast(I32),
+                    in_=rows[BLOCKS + PACK * q : BLOCKS + PACK * (q + 1), :].bitcast(I32),
+                )
 
         def by_lines(rows):
             return rows.rearrange("p j (c i) -> p c j i", i=LINE_WORDS)
@@ -84,13 +96,15 @@ def tile_picked_dime_none_po_kernel(
                 in_=raw[:].rearrange("p (r i t) -> p r t i", t=PACK, i=run),
             )
 
-        def quantize_into(codes, scales, grouped):
+        def quantize(codes, scales, grouped):
             nc.vector.quantize_mx(out=codes.bitcast(FP8X4), scales=scales, in_=grouped.rearrange("p c j -> p (c j)"))
 
-        def quantize(grouped, columns, name):
-            codes = tile([P, columns], U32, name + "_codes")
-            scales = tile([P, columns], U8, name + "_scales")
-            quantize_into(codes[:], scales[:], grouped[:])
+        def quantize_weight(grouped, name):
+            codes = tile([P, H], U32, name + "_codes")
+            scales = tile([P, H], U8, name + "_scales")
+            for pair in range(PACK // 2):
+                places = slice(pair * 2 * P, (pair + 1) * 2 * P)
+                quantize(codes[:, places], scales[:, places], grouped[:, places, :])
             return codes, scales
 
         def product(out, w_codes, w_scales, t, codes, scales):
@@ -105,40 +119,12 @@ def tile_picked_dime_none_po_kernel(
                 stop=True,
             )
 
-        def products_to_sbuf(held, w_codes, w_scales, codes, scales):
-            for pair in range(PACK // 2):
-                acc = bank([P, 2, held.shape[2]])
-                for u in range(2):
-                    product(acc[:, u, :], w_codes, w_scales, 2 * pair + u, codes, scales)
-                nc.scalar.copy(out=held[:, 2 * pair : 2 * pair + 2, :], in_=acc[:])
-
-        def load_scale_rows(src, columns, name, pool, queue):
-            rows = tile([P, columns], U8, name, pool)
-            queue.dma_start(out=rows[BLOCKS : 2 * BLOCKS, :].bitcast(I32), in_=src[0].bitcast(I32))
-            for p0, p1 in ((0, BLOCKS), (QUADRANT, 2 * QUADRANT), (2 * QUADRANT, P)):
-                nc.vector.memset(rows[p0:p1, :].bitcast(I32), 0)
-            return rows
-
-        def place_scale_rows(scales, rows):
-            for q in range(BLOCKS // PACK):
-                nc.sync.dma_start(
-                    out=scales[QUADRANT * q : QUADRANT * q + PACK, :].bitcast(I32),
-                    in_=rows[BLOCKS + PACK * q : BLOCKS + PACK * (q + 1), :].bitcast(I32),
-                )
-
-        def load_row_pairs(pool, src, name):
-            rows = src.rearrange("(p j) c -> p j c", j=PACK)
-            raws = []
-            for g in range(2):
-                raws.append(tile([P, 2, src.shape[1]], F32, "%s%d" % (name, g), pool))
-                nc.sync.dma_start(out=raws[g][:], in_=rows[:, 2 * g : 2 * g + 2, :])
-            return raws
-
         with tc.tile_pool(name="first", bufs=1) as first:
-            xs_all = load_scale_rows(x_scales, T, "xs_all", first, nc.scalar)
+            xs_all = load_scale_rows(x_scales, T, "xs_all", first)
             offs_t = load_list(offs, S, "offs_t")
-            w1_raw = load_rows(sb, w1, slice(0, H), "w1_raw")
-            w2s_raw = load_scale_rows(w2_scales, H, "w2s_raw", sb, nc.scalar)
+            w1_raw = tile([P, PACK, H], F32, "w1_raw")
+            nc.sync.dma_start(out=w1_raw[:], in_=w1.rearrange("(p j) c -> p j c", j=PACK))
+            w2s_raw = load_scale_rows(w2_scales, H, "w2s_raw", sb)
             pos_t = [load_list(pos1, V, "pos1_t")]
             xw_all = load_words(sb, x_words, T, "xw_all")
             pos_t.append(load_list(pos2, V, "pos2_t"))
@@ -164,15 +150,12 @@ def tile_picked_dime_none_po_kernel(
         deal(w2s_dealt, w2s_raw, LINE_BYTES)
         place_scale_rows(w2_sc, w2s_dealt)
 
-        def quantize_pairs(grouped, name):
-            codes = tile([P, H], U32, name + "_codes")
-            scales = tile([P, H], U8, name + "_scales")
-            for pair in range(2):
-                cols = slice(pair * 2 * P, (pair + 1) * 2 * P)
-                quantize_into(codes[:, cols], scales[:, cols], grouped[:, cols, :])
-            return codes, scales
-
-        w1_codes, w1_scales = quantize_pairs(round_dealt(w1_raw, "w1"), "w1")
+        w1_bf = tile([P, H, PACK], BF16, "w1_bf")
+        w1_dealt = w1_bf[:].rearrange("p (t m) j -> p m t j", t=PACK)
+        w1_source = w1_raw[:].rearrange("p j (m t) -> p m t j", t=PACK)
+        nc.vector.tensor_copy(out=w1_dealt[:, :VECTOR_GROUPS], in_=w1_source[:, :VECTOR_GROUPS])
+        nc.scalar.copy(out=w1_dealt[:, VECTOR_GROUPS:], in_=w1_source[:, VECTOR_GROUPS:])
+        w1_codes, w1_scales = quantize_weight(w1_bf, "w1")
 
         xw = tile([P, S], U32, "xw")
         for c0, c1 in ((0, P), (P, 2 * P), (2 * P, S)):
@@ -181,37 +164,30 @@ def tile_picked_dime_none_po_kernel(
             )
 
         h = [tile([P, S], F32, "h%d" % t) for t in range(PACK)]
-        for t, c0, c1 in (
-            [(0, 0, P), (1, 0, P), (0, P, 2 * P), (1, P, 2 * P), (2, 0, 2 * P), (3, 0, 2 * P)]
-            + [(t, 2 * P, S) for t in range(PACK)]
-        ):
-            entries = slice(c0, c1)
-            acc = bank([P, c1 - c0])
+        h_pieces = (
+            [(t, slice(c0, c0 + P)) for c0 in (0, P) for t in LOW_SLOTS]
+            + [(t, slice(0, 2 * P)) for t in HIGH_SLOTS]
+            + [(t, slice(2 * P, S)) for t in range(PACK)]
+        )
+        for n, (t, entries) in enumerate(h_pieces):
+            acc = bank([P, entries.stop - entries.start], n % PSUM_BANKS)
             product(acc[:], w1_codes, w1_scales, t, xw[:, entries], xs[:, entries])
             nc.scalar.activation(out=h[t][:, entries], in_=acc[:], func=SILU)
 
-        picked = [tile([P, 2, 2, V], F32, "picked%d" % pair) for pair in range(2)]
-
-        first_half, third_quarter, last_quarter = slice(0, P), slice(P, P + P // 2), slice(P + P // 2, V)
-        second_half = slice(P, V)
-
-        def gather(t, targets, on_vector=False):
-            for d in range(2):
-                out = picked[t // 2][:, t % 2, d, targets]
-                window = h[t][:].indirect(pos_t[d][:, targets.start // STRIPE : targets.stop // STRIPE])
-                if on_vector:
-                    nc.vector.tensor_copy(out=out, in_=window)
-                else:
-                    nc.scalar.activation(out=out, in_=window, func=COPY)
-
+        picked = [tile([P, 2, NEIGHBOURS, V], F32, "picked%d" % pair) for pair in range(PACK // 2)]
         for slots, targets in (
-            (range(PACK), first_half),
-            ((0, 1), second_half),
-            ((2, 3), third_quarter),
-            ((2, 3), last_quarter),
+            (range(PACK), FIRST_HALF),
+            (LOW_SLOTS, SECOND_HALF),
+            (HIGH_SLOTS, THIRD_QUARTER),
+            (HIGH_SLOTS, LAST_QUARTER),
         ):
             for t in slots:
-                gather(t, targets)
+                for d in range(NEIGHBOURS):
+                    nc.scalar.activation(
+                        out=picked[t // 2][:, t % 2, d, targets],
+                        in_=h[t][:].indirect(pos_t[d][:, targets.start // STRIPE : targets.stop // STRIPE]),
+                        func=COPY,
+                    )
 
         w3_bf = tile([P, H, PACK], BF16, "w3_bf")
         for g in range(2):
@@ -219,109 +195,126 @@ def tile_picked_dime_none_po_kernel(
                 out=w3_bf[:, :, 2 * g : 2 * g + 2].rearrange("p (t r i) j -> p r t i j", t=PACK, i=2),
                 in_=w3_raw[g][:].rearrange("p j (r i t) -> p r t i j", t=PACK, i=2),
             )
-        w3_codes, w3_scales = quantize_pairs(w3_bf, "w3")
+        w3_codes, w3_scales = quantize_weight(w3_bf, "w3")
 
         a_bf = tile([P, 2, V, PACK], BF16, "a_bf")
         a_codes = [tile([P, V], U32, "a_codes%d" % half) for half in range(2)]
         a_scales = [tile([P, V], U8, "a_scales%d" % half) for half in range(2)]
 
-        def round_angles(g, half):
-            pieces = 1 + half
-            nc.vector.tensor_copy(
-                out=a_bf[:, half, :, 2 * g : 2 * g + 2].rearrange("p (q d c) j -> p q d c j", q=pieces, d=2),
-                in_=a_raw[g][:].rearrange("p j (d u q c) -> p u q d c j", d=2, u=2, q=pieces)[:, half],
-            )
+        def round_angles(g, half, neighbours):
+            pieces = (1, 2)[half]
+            out = a_bf[:, half, :, 2 * g : 2 * g + 2].rearrange("p (q d c) j -> p q d c j", q=pieces, d=NEIGHBOURS)
+            rows = a_raw[g][:].rearrange("p j (d u q c) -> p u q d c j", d=NEIGHBOURS, u=2, q=pieces)[:, half]
+            nc.vector.tensor_copy(out=out[:, :, neighbours], in_=rows[:, :, neighbours])
 
-        def quantize_angles(half):
-            quantize_into(a_codes[half][:], a_scales[half][:], a_bf[:, half])
+        def quantize_angles(half, columns):
+            quantize(a_codes[half][:, columns], a_scales[half][:, columns], a_bf[:, half, columns])
 
-        for g in range(2):
-            for half in range(2):
-                round_angles(g, half)
         for half in range(2):
-            quantize_angles(half)
+            round_angles(0, half, slice(0, NEIGHBOURS))
+        for d in range(NEIGHBOURS):
+            round_angles(1, 0, slice(d, d + 1))
+        for d in range(NEIGHBOURS):
+            quantize_angles(0, slice(d * P, (d + 1) * P))
+        round_angles(1, 1, slice(0, NEIGHBOURS))
+        w2_codes = tile([P, H], I32, "w2_codes")
+        deal(w2_codes, w2w_raw, LINE_WORDS)
+        quantize_angles(1, slice(0, V))
 
         y_codes = tile([P, V], I32, "y_codes")
         y_scales = tile([P, V], U8, "y_scales")
-        rows_out = out_0.rearrange("(p t) v -> p t v", t=PACK)
-        words_out = out_1[0].rearrange("p c r -> p (c r)").bitcast(I32)
-        terms = tile([P, PACK, 2, V], F32, "terms")
-        zb = tile([P, V, PACK], BF16, "z_bf")
+        terms = tile([P, PACK, NEIGHBOURS, V], F32, "terms")
+        z_bf = tile([P, V, PACK], BF16, "z_bf")
         z_codes = tile([P, V], U32, "z_codes")
         z_scales = tile([P, V], U8, "z_scales")
 
-        def multiply(slots, targets, tag, warm_up=False):
-            half, n = targets.start // P, targets.stop - targets.start
-            cols = slice(2 * (targets.start - half * P), 2 * (targets.stop - half * P))
-            whole = psum_f.tile([P, 2 * V], F32, name="filters", tag=tag)
-            acc = whole[:, : len(slots) * 2 * n].rearrange("p (t c) -> p t c", t=len(slots))
+        def make_filters(slots, targets, number):
+            half, width = targets.start // P, NEIGHBOURS * (targets.stop - targets.start)
+            c0 = NEIGHBOURS * (targets.start - half * P)
+            columns = slice(c0, c0 + width)
+            acc = bank([P, 2 * V], number)
             for u, t in enumerate(slots):
-                product(acc[:, u, :], w3_codes, w3_scales, t, a_codes[half][:, cols], a_scales[half][:, cols])
-            if warm_up:
-                for t in slots:
-                    product(whole[:, V:], w3_codes, w3_scales, t, a_codes[0][:], a_scales[0][:])
-            u0 = slots[0] % 2
+                out = acc[:, u * width : (u + 1) * width]
+                product(out, w3_codes, w3_scales, t, a_codes[half][:, columns], a_scales[half][:, columns])
+            return acc
+
+        def multiply(acc, slots, targets):
+            u0, count = slots[0] % 2, len(slots) * NEIGHBOURS * (targets.stop - targets.start)
             nc.vector.tensor_tensor(
                 out=terms[:, slots[0] : slots[-1] + 1, :, targets],
                 in0=picked[slots[0] // 2][:, u0 : u0 + len(slots), :, targets],
-                in1=acc.rearrange("p t (d v) -> p t d v", d=2),
+                in1=acc[:, :count].rearrange("p (t d v) -> p t d v", t=len(slots), d=NEIGHBOURS),
                 op=MULT,
             )
 
+        def filter_terms(slots, targets, number):
+            multiply(make_filters(slots, targets, number), slots, targets)
+
         def add_terms(targets):
             nc.vector.tensor_tensor(
-                out=woven(zb[:, targets, :]),
+                out=woven(z_bf[:, targets, :]),
                 in0=by_lines(terms[:, :, 0, targets]),
                 in1=by_lines(terms[:, :, 1, targets]),
                 op=ADD,
             )
 
         def quantize_z(targets):
-            quantize_into(z_codes[:, targets], z_scales[:, targets], zb[:, targets, :])
+            quantize(z_codes[:, targets], z_scales[:, targets], z_bf[:, targets, :])
 
-        w2_codes = tile([P, H], I32, "w2_codes")
-        deal(w2_codes, w2w_raw, LINE_WORDS)
-        multiply((0,), first_half, "low")
-        multiply((1,), first_half, "second")
-        multiply((2, 3), first_half, "high")
-        multiply((0, 1), third_quarter, "low")
-        add_terms(first_half)
-        multiply((2, 3), third_quarter, "high")
-        quantize_z(first_half)
-        multiply((0, 1), last_quarter, "low", warm_up=True)
-        add_terms(third_quarter)
-        multiply((2, 3), last_quarter, "high")
-        quantize_z(third_quarter)
-        add_terms(last_quarter)
-        quantize_z(last_quarter)
+        def warm_up(out, t):
+            product(out, w3_codes, w3_scales, t, a_codes[0][:], a_scales[0][:])
+
+        for t in range(PACK):
+            filter_terms((t,), FIRST_HALF, FILTER_BANK + t)
+        filter_terms(LOW_SLOTS, THIRD_QUARTER, LOW_BANK)
+        add_terms(FIRST_HALF)
+        filter_terms(HIGH_SLOTS, THIRD_QUARTER, HIGH_BANK)
+        quantize_z(FIRST_HALF)
+        acc = make_filters(LOW_SLOTS, LAST_QUARTER, LOW_BANK)
+        warm_up(acc[:, V:], 0)
+        multiply(acc, LOW_SLOTS, LAST_QUARTER)
+        warm_up(bank([P, 2 * V], LOW_BANK)[:, :V], 1)
+        add_terms(THIRD_QUARTER)
+        filter_terms(HIGH_SLOTS, LAST_QUARTER, HIGH_BANK)
+        quantize_z(THIRD_QUARTER)
+        add_terms(LAST_QUARTER)
+        quantize_z(LAST_QUARTER)
 
         y = [tile([P, PACK, P], F32, "y%d" % half) for half in range(2)]
-        yb = tile_over("terms", [P, V, PACK], BF16, "y_bf")
-        products_to_sbuf(y[0], w2_codes, w2_sc, z_codes[:, first_half], z_scales[:, first_half])
-        nc.sync.dma_start(out=rows_out[:, :, first_half], in_=y[0][:])
-        nc.vector.tensor_copy(out=woven(yb[:, first_half, :]), in_=by_lines(y[0][:]))
-        acc = bank([P, PACK, P // 2])
-        for t in range(PACK):
-            product(acc[:, t, :], w2_codes, w2_sc, t, z_codes[:, third_quarter], z_scales[:, third_quarter])
-        nc.scalar.copy(out=y[1][:, :, : P // 2], in_=acc[:])
-        products_to_sbuf(y[1][:, :, P // 2 :], w2_codes, w2_sc, z_codes[:, last_quarter], z_scales[:, last_quarter])
-        nc.sync.dma_start(out=rows_out[:, :, second_half], in_=y[1][:])
+        y_bf = sb.tile([P, V, PACK], BF16, name="y_bf", tag="terms", align_bytes=64)
+        rows_out = out_0.rearrange("(p t) v -> p t v", t=PACK)
+        words_out = out_1[0].rearrange("p c r -> p (c r)").bitcast(I32)
+
+        def y_piece(targets):
+            half = targets.start // P
+            return y[half][:, :, targets.start - half * P : targets.stop - half * P]
+
+        def last_product(targets, slot_groups, first_bank):
+            for n, slots in enumerate(slot_groups):
+                acc = bank([P, len(slots), targets.stop - targets.start], first_bank + n)
+                for u, t in enumerate(slots):
+                    product(acc[:, u, :], w2_codes, w2_sc, t, z_codes[:, targets], z_scales[:, targets])
+                nc.scalar.copy(out=y_piece(targets)[:, slots[0] : slots[-1] + 1, :], in_=acc[:])
 
         def round_y(targets):
-            nc.vector.tensor_copy(
-                out=woven(yb[:, targets, :]), in_=by_lines(y[1][:, :, targets.start - P : targets.stop - P])
-            )
+            nc.vector.tensor_copy(out=woven(y_bf[:, targets, :]), in_=by_lines(y_piece(targets)))
 
         def quantize_y(targets):
-            quantize_into(y_codes[:, targets], y_scales[:, targets], yb[:, targets, :])
+            quantize(y_codes[:, targets], y_scales[:, targets], y_bf[:, targets, :])
 
-        round_y(third_quarter)
-        quantize_y(first_half)
-        nc.sync.dma_start(out=words_out[:, first_half], in_=y_codes[:, first_half])
-        quantize_y(third_quarter)
-        round_y(last_quarter)
-        quantize_y(last_quarter)
-        nc.sync.dma_start(out=words_out[:, second_half], in_=y_codes[:, second_half])
+        last_product(FIRST_HALF, (LOW_SLOTS, HIGH_SLOTS), FIRST_HALF_BANK)
+        nc.sync.dma_start(out=rows_out[:, :, FIRST_HALF], in_=y[0][:])
+        round_y(FIRST_HALF)
+        last_product(THIRD_QUARTER, (LOW_SLOTS + HIGH_SLOTS,), THIRD_QUARTER_BANK)
+        last_product(LAST_QUARTER, (LOW_SLOTS, HIGH_SLOTS), LAST_QUARTER_BANK)
+        nc.sync.dma_start(out=rows_out[:, :, SECOND_HALF], in_=y[1][:])
+        round_y(THIRD_QUARTER)
+        quantize_y(FIRST_HALF)
+        nc.sync.dma_start(out=words_out[:, FIRST_HALF], in_=y_codes[:, FIRST_HALF])
+        quantize_y(THIRD_QUARTER)
+        round_y(LAST_QUARTER)
+        quantize_y(LAST_QUARTER)
+        nc.sync.dma_start(out=words_out[:, SECOND_HALF], in_=y_codes[:, SECOND_HALF])
         for q in range(BLOCKS // PACK):
             queue = nc.scalar if q == 0 else nc.sync
             queue.dma_start(

from contextlib import ExitStack

import concourse.mybir as mybir

K, T, S, V, H, J, U = 512, 2048, 512, 256, 512, 512, 512
FLOPS = 2 * K * H * S + 2 * J * H * U + 2 * H * H * V

F32 = mybir.dt.float32
BF16 = mybir.dt.bfloat16
I32 = mybir.dt.int32
U32 = mybir.dt.uint32
U16 = mybir.dt.uint16
U8 = mybir.dt.uint8
FP8X4 = mybir.dt.float8_e4m3fn_x4
MULT = mybir.AluOpType.mult
ADD = mybir.AluOpType.add
SILU = mybir.ActivationFunctionType.Silu
COPY = mybir.ActivationFunctionType.Copy

P = 128
PACK = 4
NEIGHBOURS = 2
BLOCKS = 16
QUADRANT = 32
STRIPE = 16
LINE_WORDS = 4
LINE_BYTES = 16
VECTOR_GROUPS = 84

LOW_SLOTS, HIGH_SLOTS = (0, 1), (2, 3)
FIRST_HALF, SECOND_HALF = slice(0, P), slice(P, V)
THIRD_QUARTER, LAST_QUARTER = slice(P, P + P // 2), slice(P + P // 2, V)

PSUM_BANKS = 8
FILTER_BANK = 2
LOW_BANK, HIGH_BANK = FILTER_BANK, FILTER_BANK + PACK - 1
FIRST_HALF_BANK, THIRD_QUARTER_BANK, LAST_QUARTER_BANK = 6, 0, 3


def tile_picked_dime_none_po_kernel(
    tc, x_words, x_scales, aT, w1, w3, w2_words, w2_scales, offs, pos1, pos2, out_0, out_1, out_2
):
    nc = tc.nc
    with ExitStack() as ctx:
        lists = ctx.enter_context(tc.tile_pool(name="lists", bufs=1))
        sb = ctx.enter_context(tc.tile_pool(name="sb", bufs=1))
        psum = ctx.enter_context(tc.psum_pool(name="psum", bufs=1))

        def tile(shape, dtype, name, pool=sb):
            return pool.tile(shape, dtype, name=name, align_bytes=64)

        def bank(shape, number):
            return psum.tile(shape, F32, name="bank", tag="bank%d" % number)

        def load_list(src, entries, name):
            held = lists.tile([P, entries // STRIPE], U16, name=name)
            nc.sync.dma_start(held[:], src)
            return held

        def load_words(pool, src, columns, name):
            words = tile([P, columns], I32, name, pool)
            nc.sync.dma_start(out=words[:], in_=src[0].rearrange("p c r -> p (c r)").bitcast(I32))
            return words

        def load_row_pairs(pool, src, name):
            rows = src.rearrange("(p j) c -> p j c", j=PACK)
            raws = []
            for g in range(2):
                raws.append(tile([P, 2, src.shape[1]], F32, "%s%d" % (name, g), pool))
                nc.sync.dma_start(out=raws[g][:], in_=rows[:, 2 * g : 2 * g + 2, :])
            return raws

        def load_scale_rows(src, columns, name, pool):
            rows = tile([P, columns], U8, name, pool)
            nc.scalar.dma_start(out=rows[BLOCKS : 2 * BLOCKS, :].bitcast(I32), in_=src[0].bitcast(I32))
            for p0, p1 in ((0, BLOCKS), (QUADRANT, 2 * QUADRANT), (2 * QUADRANT, P)):
                nc.vector.memset(rows[p0:p1, :].bitcast(I32), 0)
            return rows

        def place_scale_rows(scales, rows):
            for q in range(BLOCKS // PACK):
                nc.sync.dma_start(
                    out=scales[QUADRANT * q : QUADRANT * q + PACK, :].bitcast(I32),
                    in_=rows[BLOCKS + PACK * q : BLOCKS + PACK * (q + 1), :].bitcast(I32),
                )

        def by_lines(rows):
            return rows.rearrange("p j (c i) -> p c j i", i=LINE_WORDS)

        def woven(grouped):
            return grouped.rearrange("p (c i) j -> p c j i", i=LINE_WORDS)

        def deal(out, raw, run):
            nc.vector.tensor_copy(
                out=out[:].rearrange("p (t r i) -> p r t i", t=PACK, i=run),
                in_=raw[:].rearrange("p (r i t) -> p r t i", t=PACK, i=run),
            )

        def quantize(codes, scales, grouped):
            nc.vector.quantize_mx(out=codes.bitcast(FP8X4), scales=scales, in_=grouped.rearrange("p c j -> p (c j)"))

        def quantize_weight(grouped, name):
            codes = tile([P, H], U32, name + "_codes")
            scales = tile([P, H], U8, name + "_scales")
            for pair in range(PACK // 2):
                places = slice(pair * 2 * P, (pair + 1) * 2 * P)
                quantize(codes[:, places], scales[:, places], grouped[:, places, :])
            return codes, scales

        def product(out, w_codes, w_scales, t, codes, scales):
            places = slice(t * P, (t + 1) * P)
            nc.tensor.matmul_mx(
                out=out,
                lhsT=w_codes[:, places].bitcast(FP8X4),
                lhsT_scale=w_scales[:, places],
                rhs=codes.bitcast(FP8X4),
                rhs_scale=scales,
                start=True,
                stop=True,
            )

        with tc.tile_pool(name="first", bufs=1) as first:
            xs_all = load_scale_rows(x_scales, T, "xs_all", first)
            offs_t = load_list(offs, S, "offs_t")
            w1_raw = tile([P, PACK, H], F32, "w1_raw")
            nc.sync.dma_start(out=w1_raw[:], in_=w1.rearrange("(p j) c -> p j c", j=PACK))
            w2s_raw = load_scale_rows(w2_scales, H, "w2s_raw", sb)
            pos_t = [load_list(pos1, V, "pos1_t")]
            xw_all = load_words(sb, x_words, T, "xw_all")
            pos_t.append(load_list(pos2, V, "pos2_t"))
            xs = tile([P, S], U8, "xs")
            nc.vector.memset(xs[:].bitcast(I32), 0)
            w2_sc = tile([P, H], U8, "w2_sc")
            nc.vector.memset(w2_sc[:].bitcast(I32), 0)

            warm_in = tile([P, 1], F32, "warm_in")
            nc.vector.memset(warm_in[:], 0.0)
            warm_out = tile([P, 1], F32, "warm_out")
            nc.scalar.activation(out=warm_out[:], in_=warm_in[:], func=SILU)

            xs_rows = tile([P, S], U8, "xs_rows")
            nc.vector.tensor_copy(out=xs_rows[:], in_=xs_all[:].indirect(offs_t[:]))
            place_scale_rows(xs, xs_rows)

        later = ctx.enter_context(tc.tile_pool(name="later", bufs=1))
        w3_raw = load_row_pairs(later, w3, "w3_raw")
        a_raw = load_row_pairs(later, aT, "a_raw")
        w2w_raw = load_words(later, w2_words, H, "w2w_raw")
        w2s_dealt = tile([P, H], U8, "w2s_dealt")
        deal(w2s_dealt, w2s_raw, LINE_BYTES)
        place_scale_rows(w2_sc, w2s_dealt)

        w1_bf = tile([P, H, PACK], BF16, "w1_bf")
        w1_dealt = w1_bf[:].rearrange("p (t m) j -> p m t j", t=PACK)
        w1_source = w1_raw[:].rearrange("p j (m t) -> p m t j", t=PACK)
        nc.vector.tensor_copy(out=w1_dealt[:, :VECTOR_GROUPS], in_=w1_source[:, :VECTOR_GROUPS])
        nc.scalar.copy(out=w1_dealt[:, VECTOR_GROUPS:], in_=w1_source[:, VECTOR_GROUPS:])
        w1_codes, w1_scales = quantize_weight(w1_bf, "w1")

        xw = tile([P, S], U32, "xw")
        for c0, c1 in ((0, P), (P, 2 * P), (2 * P, S)):
            nc.vector.tensor_copy(
                out=xw[:, c0:c1], in_=xw_all[:].bitcast(U32).indirect(offs_t[:, c0 // STRIPE : c1 // STRIPE])
            )

        h = [tile([P, S], F32, "h%d" % t) for t in range(PACK)]
        h_pieces = (
            [(t, slice(c0, c0 + P)) for c0 in (0, P) for t in LOW_SLOTS]
            + [(t, slice(0, 2 * P)) for t in HIGH_SLOTS]
            + [(t, slice(2 * P, S)) for t in range(PACK)]
        )
        for n, (t, entries) in enumerate(h_pieces):
            acc = bank([P, entries.stop - entries.start], n % PSUM_BANKS)
            product(acc[:], w1_codes, w1_scales, t, xw[:, entries], xs[:, entries])
            nc.scalar.activation(out=h[t][:, entries], in_=acc[:], func=SILU)

        picked = [tile([P, 2, NEIGHBOURS, V], F32, "picked%d" % pair) for pair in range(PACK // 2)]
        for slots, targets in (
            (range(PACK), FIRST_HALF),
            (LOW_SLOTS, SECOND_HALF),
            (HIGH_SLOTS, THIRD_QUARTER),
            (HIGH_SLOTS, LAST_QUARTER),
        ):
            for t in slots:
                for d in range(NEIGHBOURS):
                    nc.scalar.activation(
                        out=picked[t // 2][:, t % 2, d, targets],
                        in_=h[t][:].indirect(pos_t[d][:, targets.start // STRIPE : targets.stop // STRIPE]),
                        func=COPY,
                    )

        w3_bf = tile([P, H, PACK], BF16, "w3_bf")
        for g in range(2):
            nc.vector.tensor_copy(
                out=w3_bf[:, :, 2 * g : 2 * g + 2].rearrange("p (t r i) j -> p r t i j", t=PACK, i=2),
                in_=w3_raw[g][:].rearrange("p j (r i t) -> p r t i j", t=PACK, i=2),
            )
        w3_codes, w3_scales = quantize_weight(w3_bf, "w3")

        a_bf = tile([P, 2, V, PACK], BF16, "a_bf")
        a_codes = [tile([P, V], U32, "a_codes%d" % half) for half in range(2)]
        a_scales = [tile([P, V], U8, "a_scales%d" % half) for half in range(2)]

        def round_angles(g, half, neighbours):
            pieces = (1, 2)[half]
            out = a_bf[:, half, :, 2 * g : 2 * g + 2].rearrange("p (q d c) j -> p q d c j", q=pieces, d=NEIGHBOURS)
            rows = a_raw[g][:].rearrange("p j (d u q c) -> p u q d c j", d=NEIGHBOURS, u=2, q=pieces)[:, half]
            nc.vector.tensor_copy(out=out[:, :, neighbours], in_=rows[:, :, neighbours])

        def quantize_angles(half, columns):
            quantize(a_codes[half][:, columns], a_scales[half][:, columns], a_bf[:, half, columns])

        for half in range(2):
            round_angles(0, half, slice(0, NEIGHBOURS))
        for d in range(NEIGHBOURS):
            round_angles(1, 0, slice(d, d + 1))
        for d in range(NEIGHBOURS):
            quantize_angles(0, slice(d * P, (d + 1) * P))
        round_angles(1, 1, slice(0, NEIGHBOURS))
        w2_codes = tile([P, H], I32, "w2_codes")
        deal(w2_codes, w2w_raw, LINE_WORDS)
        quantize_angles(1, slice(0, V))

        y_codes = tile([P, V], I32, "y_codes")
        y_scales = tile([P, V], U8, "y_scales")
        terms = tile([P, PACK, NEIGHBOURS, V], F32, "terms")
        z_bf = tile([P, V, PACK], BF16, "z_bf")
        z_codes = tile([P, V], U32, "z_codes")
        z_scales = tile([P, V], U8, "z_scales")

        def make_filters(slots, targets, number):
            half, width = targets.start // P, NEIGHBOURS * (targets.stop - targets.start)
            c0 = NEIGHBOURS * (targets.start - half * P)
            columns = slice(c0, c0 + width)
            acc = bank([P, 2 * V], number)
            for u, t in enumerate(slots):
                out = acc[:, u * width : (u + 1) * width]
                product(out, w3_codes, w3_scales, t, a_codes[half][:, columns], a_scales[half][:, columns])
            return acc

        def multiply(acc, slots, targets):
            u0, count = slots[0] % 2, len(slots) * NEIGHBOURS * (targets.stop - targets.start)
            nc.vector.tensor_tensor(
                out=terms[:, slots[0] : slots[-1] + 1, :, targets],
                in0=picked[slots[0] // 2][:, u0 : u0 + len(slots), :, targets],
                in1=acc[:, :count].rearrange("p (t d v) -> p t d v", t=len(slots), d=NEIGHBOURS),
                op=MULT,
            )

        def filter_terms(slots, targets, number):
            multiply(make_filters(slots, targets, number), slots, targets)

        def add_terms(targets):
            nc.vector.tensor_tensor(
                out=woven(z_bf[:, targets, :]),
                in0=by_lines(terms[:, :, 0, targets]),
                in1=by_lines(terms[:, :, 1, targets]),
                op=ADD,
            )

        def quantize_z(targets):
            quantize(z_codes[:, targets], z_scales[:, targets], z_bf[:, targets, :])

        def warm_up(out, t):
            product(out, w3_codes, w3_scales, t, a_codes[0][:], a_scales[0][:])

        for t in range(PACK):
            filter_terms((t,), FIRST_HALF, FILTER_BANK + t)
        filter_terms(LOW_SLOTS, THIRD_QUARTER, LOW_BANK)
        add_terms(FIRST_HALF)
        filter_terms(HIGH_SLOTS, THIRD_QUARTER, HIGH_BANK)
        quantize_z(FIRST_HALF)
        acc = make_filters(LOW_SLOTS, LAST_QUARTER, LOW_BANK)
        warm_up(acc[:, V:], 0)
        multiply(acc, LOW_SLOTS, LAST_QUARTER)
        warm_up(bank([P, 2 * V], LOW_BANK)[:, :V], 1)
        add_terms(THIRD_QUARTER)
        filter_terms(HIGH_SLOTS, LAST_QUARTER, HIGH_BANK)
        quantize_z(THIRD_QUARTER)
        add_terms(LAST_QUARTER)
        quantize_z(LAST_QUARTER)

        y = [tile([P, PACK, P], F32, "y%d" % half) for half in range(2)]
        y_bf = sb.tile([P, V, PACK], BF16, name="y_bf", tag="terms", align_bytes=64)
        rows_out = out_0.rearrange("(p t) v -> p t v", t=PACK)
        words_out = out_1[0].rearrange("p c r -> p (c r)").bitcast(I32)

        def y_piece(targets):
            half = targets.start // P
            return y[half][:, :, targets.start - half * P : targets.stop - half * P]

        def last_product(targets, slot_groups, first_bank):
            for n, slots in enumerate(slot_groups):
                acc = bank([P, len(slots), targets.stop - targets.start], first_bank + n)
                for u, t in enumerate(slots):
                    product(acc[:, u, :], w2_codes, w2_sc, t, z_codes[:, targets], z_scales[:, targets])
                nc.scalar.copy(out=y_piece(targets)[:, slots[0] : slots[-1] + 1, :], in_=acc[:])

        def round_y(targets):
            nc.vector.tensor_copy(out=woven(y_bf[:, targets, :]), in_=by_lines(y_piece(targets)))

        def quantize_y(targets):
            quantize(y_codes[:, targets], y_scales[:, targets], y_bf[:, targets, :])

        last_product(FIRST_HALF, (LOW_SLOTS, HIGH_SLOTS), FIRST_HALF_BANK)
        nc.sync.dma_start(out=rows_out[:, :, FIRST_HALF], in_=y[0][:])
        round_y(FIRST_HALF)
        last_product(THIRD_QUARTER, (LOW_SLOTS + HIGH_SLOTS,), THIRD_QUARTER_BANK)
        last_product(LAST_QUARTER, (LOW_SLOTS, HIGH_SLOTS), LAST_QUARTER_BANK)
        nc.sync.dma_start(out=rows_out[:, :, SECOND_HALF], in_=y[1][:])
        round_y(THIRD_QUARTER)
        quantize_y(FIRST_HALF)
        nc.sync.dma_start(out=words_out[:, FIRST_HALF], in_=y_codes[:, FIRST_HALF])
        quantize_y(THIRD_QUARTER)
        round_y(LAST_QUARTER)
        quantize_y(LAST_QUARTER)
        nc.sync.dma_start(out=words_out[:, SECOND_HALF], in_=y_codes[:, SECOND_HALF])
        for q in range(BLOCKS // PACK):
            queue = nc.scalar if q == 0 else nc.sync
            queue.dma_start(
                out=out_2[0, PACK * q : PACK * (q + 1), :].bitcast(I32),
                in_=y_scales[QUADRANT * q : QUADRANT * q + PACK, :].bitcast(I32),
            )
